import numpy as np
import ml_dtypes


def mxq(x, axis, fmt="e4m3"):
    dtype, down = {"e4m3": (ml_dtypes.float8_e4m3fn, 7), "e5m2": (ml_dtypes.float8_e5m2, 14)}[fmt]
    v = np.moveaxis(np.asarray(x, np.float32).astype(ml_dtypes.bfloat16).astype(np.float64), axis, -1)
    blocks = v.reshape(v.shape[:-1] + (-1, 32))
    amax = np.abs(blocks).max(-1, keepdims=True)
    byte = np.maximum(np.where(amax > 0, np.frexp(amax)[1] - 1 + 127, 0) - down, 1)
    scale = np.exp2(byte - 127.0)
    codes = (blocks / scale).astype(np.float32).astype(dtype).astype(np.float64)
    return np.moveaxis((codes * scale).reshape(v.shape), -1, axis)


WIDE = False


def mx_kscale(k):
    if not WIDE:
        return np.ones(k)
    levels = np.array([10, -10, 5, -5, 0])
    if k % 512:
        return np.exp2(np.random.permutation(np.resize(levels, k // 32))).repeat(32)
    a = np.empty((k // 512, 16))
    for p in range(k // 512):
        a[p, :8] = np.random.permutation(np.resize(levels, 8))
        for g in range(8):
            far = levels[np.abs(levels - a[p, g]) >= 10]
            a[p, g + 8] = far[np.random.randint(len(far))]
    return np.exp2(a.ravel()).repeat(32)


def f64(x):
    return np.asarray(x).astype(np.float64)


def striped(idx):
    return np.tile(idx.reshape(-1, 16).T, (8, 1)).astype(np.uint16)


def unstriped(offs):
    return offs[:16].T.reshape(-1).astype(np.int64)


E2M1 = np.array([0.0, 0.5, 1.0, 1.5, 2.0, 3.0, 4.0, 6.0, -0.0, -0.5, -1.0, -1.5, -2.0, -3.0, -4.0, -6.0])


def pack_weight(w, fmt):
    k, n = w.shape
    w = f64(np.asarray(w, np.float32).astype(ml_dtypes.bfloat16)).reshape(k // 32, 32, n)
    amax = np.abs(w).max(1)
    if fmt == "e4m3":
        byte = np.frexp(amax)[1] - 1 + 127 - 7
    else:
        mant, ex = np.frexp(amax / 6.0)
        byte = np.where(mant > 0.5, ex, ex - 1) + 127
    byte = np.clip(np.where(amax > 0, byte, 1), 1, 254)
    scaled = (w * np.exp2(127.0 - byte)[:, None, :]).reshape(k, n).astype(np.float32)
    by_word = np.ascontiguousarray(scaled.reshape(k // 512, 128, 4, n).transpose(0, 1, 3, 2))
    if fmt == "e4m3":
        words = by_word.astype(ml_dtypes.float8_e4m3fn).view(np.uint8)
    else:
        c = by_word.astype(ml_dtypes.float4_e2m1fn).view(np.uint8) & 0xF
        words = (c[..., 0::2] | (c[..., 1::2] << 4)).reshape(k // 512, 128, 2 * n)
    return np.ascontiguousarray(words), np.ascontiguousarray(byte.astype(np.uint8).reshape(k // 512, 16, n))


def unpack_weight(words, scales, fmt):
    g, _, n = scales.shape
    words = np.ascontiguousarray(words).reshape(g, 128, n, -1)
    if fmt == "e4m3":
        vals = words.view(ml_dtypes.float8_e4m3fn).astype(np.float64)
    else:
        nib = np.empty((g, 128, n, 4), np.uint8)
        nib[..., 0::2] = words & 0xF
        nib[..., 1::2] = words >> 4
        vals = E2M1[nib]
    vals = vals * np.repeat(np.exp2(scales.astype(np.float64) - 127.0), 8, axis=1)[..., None]
    return vals.transpose(0, 1, 3, 2).reshape(g * 512, n)


def gelu(v):
    return 0.5 * v * (1.0 + np.tanh(np.sqrt(2.0 / np.pi) * (v + 0.044715 * v**3)))


K, T, S, T2, S2, N = 1024, 4096, 1024, 2048, 512, 768


def setup_inputs():
    n = np.random.standard_normal
    s = mx_kscale(K)[:, None]
    u = mx_kscale(S)
    tab_words, tab_scales = pack_weight(n((K, T)) * s, "e4m3")
    tab2_words, tab2_scales = pack_weight(n((K, T2)) * 2.0 / np.sqrt(K) / s, "e4m3")
    w4_words, w4_scales = pack_weight(n((S, N)) * 2.0 / np.sqrt(S) / u[:, None], "e2m1")
    wg = (n((S, N)) * 3.0 / np.sqrt(S) / u[:, None]).astype(np.float32)
    conf = (np.random.uniform(0.3, 1.0, S) * u).astype(np.float32)
    offs = striped(np.random.permutation(T)[:S])
    offs2 = striped(np.random.permutation(T2)[:S2])
    return {"tab_words": tab_words, "tab_scales": tab_scales,
            "tab2_words": tab2_words, "tab2_scales": tab2_scales,
            "w4_words": w4_words, "w4_scales": w4_scales,
            "wg": wg, "conf": conf, "offs": offs, "offs2": offs2}


def reference(tab_words, tab_scales, tab2_words, tab2_scales, w4_words, w4_scales,
              wg, conf, offs, offs2):
    v = unpack_weight(tab_words, tab_scales, "e4m3")[:, unstriped(offs)]
    v2 = unpack_weight(tab2_words, tab2_scales, "e4m3")[:, unstriped(offs2)]
    a = v.T @ v2
    h = f64(conf)[:, None] * (1.0 / (1.0 + np.exp(-a)))
    hq = mxq(h, 0, "e4m3")
    w4 = unpack_weight(w4_words, w4_scales, "e2m1")
    c = w4.T @ hq
    g = mxq(f64(wg), 0, "e4m3").T @ hq
    return c * (1.0 / (1.0 + np.exp(-g)))

@@ -1,0 +1,244 @@
+from contextlib import ExitStack
+
+import concourse.mybir as mybir
+
+K, T, S, T2, S2, N = 1024, 4096, 1024, 2048, 512, 768
+FLOPS = 2 * K * S * S2 + 2 * 2 * S * N * S2
+
+F32 = mybir.dt.float32
+BF16 = mybir.dt.bfloat16
+I32 = mybir.dt.int32
+U32 = mybir.dt.uint32
+U16 = mybir.dt.uint16
+U8 = mybir.dt.uint8
+FP8X4 = mybir.dt.float8_e4m3fn_x4
+FP4X4 = mybir.dt.float4_e2m1fn_x4
+SIGMOID = mybir.ActivationFunctionType.Sigmoid
+MULT = mybir.AluOpType.mult
+
+P = 128
+PACK = 4
+PASSES = 2
+QUADS = 4
+HALF = 256
+WG_CHUNKS = ((0, 256), (256, 256), (512, 128), (640, 128))
+SHARES = {
+    "keys0": "key_sc_list",
+    "keys1": "query_tab_sc",
+    "queries1": "key_tab1",
+    "wb0_0": "query_tab1",
+    "wb0_1": "sig0_0",
+    "wb1_0": "sig0_1",
+    "wb1_1": "hb0_0",
+    "wb2_0": "hb0_1",
+    "wb2_1": "sig1_0",
+    "wb3_0": "sig1_1",
+    "wb3_1": "hb1_0",
+}
+
+
+def tile_list_beam_sigmoid_glu_kernel(tc, tab_words, tab_scales, tab2_words, tab2_scales,
+                                               w4_words, w4_scales, wg, conf, offs, offs2, out):
+    nc = tc.nc
+    with ExitStack() as ctx:
+        keep = ctx.enter_context(tc.tile_pool(name="keep", bufs=1))
+        psum = ctx.enter_context(tc.psum_pool(name="psum", bufs=8))
+
+        def tile(name, shape, dtype):
+            return keep.tile(shape, dtype, name=name, tag=SHARES.get(name, name), align_bytes=64)
+
+        key_list = keep.tile([P, S // 16], U16, name="key_list")
+        query_list = keep.tile([P, S2 // 16], U16, name="query_list")
+        key_tab = [tile("key_tab%d" % a, [P, T], I32) for a in range(PASSES)]
+        query_tab = [tile("query_tab%d" % a, [P, T2], I32) for a in range(PASSES)]
+        key_tab_sc = tile("key_tab_sc", [P, T // 4], I32)
+        query_tab_sc = tile("query_tab_sc", [P, T2 // 4], I32)
+        w4_sc = tile("w4_sc", [P, PASSES, N // 4], I32)
+        w4_w = tile("w4_w", [P, PASSES, N // 2], I32)
+        conf_sb = tile("conf_sb", [P, PASSES, PACK], F32)
+
+        nc.vector.memset(key_tab_sc[:], 0)
+        nc.vector.memset(query_tab_sc[:], 0)
+        nc.vector.memset(w4_sc[:], 0)
+
+        for q in range(QUADS):
+            nc.gpsimd.dma_start(out=key_tab_sc[32 * q: 32 * q + 8, :],
+                                in_=tab_scales[:, 4 * q: 4 * q + 4, :].bitcast(I32))
+        for q in range(QUADS):
+            nc.gpsimd.dma_start(out=query_tab_sc[32 * q + 8: 32 * q + 16, :],
+                                in_=tab2_scales[:, 4 * q: 4 * q + 4, :].bitcast(I32))
+
+        nc.sync.dma_start(query_list[:], offs2)
+        nc.sync.dma_start(key_list[:], offs)
+
+        def load_words(dst, words):
+            nc.sync.dma_start(out=dst[:], in_=words.rearrange("p t i -> p (t i)").bitcast(I32))
+
+        load_words(query_tab[0], tab2_words[0])
+        load_words(key_tab[0], tab_words[0])
+        load_words(key_tab[1], tab_words[1])
+        load_words(query_tab[1], tab2_words[1])
+
+        wg_raw = {}
+
+        def load_wg(c):
+            n0, width = WG_CHUNKS[c]
+            for b in range(PASSES):
+                wg_raw[c, b] = tile("wg_raw%d_%d" % (c, b), [P, PACK, width], F32)
+                nc.sync.dma_start(out=wg_raw[c, b][:],
+                                  in_=wg[512 * b: 512 * (b + 1), n0: n0 + width].rearrange("(p t) n -> p t n", t=PACK))
+
+        nc.sync.dma_start(out=conf_sb[:], in_=conf.rearrange("(b p t) -> p b t", b=PASSES, t=PACK))
+        load_wg(0)
+        nc.sync.dma_start(out=w4_w[:], in_=w4_words.rearrange("a p e -> p a e").bitcast(I32))
+        for q in range(QUADS):
+            nc.sync.dma_start(out=w4_sc[32 * q: 32 * q + 4, :, :],
+                              in_=w4_scales[:, 4 * q: 4 * q + 4, :].rearrange("a r n -> r a n").bitcast(I32))
+        for c in range(1, len(WG_CHUNKS)):
+            load_wg(c)
+
+        def gather_queries(a):
+            dst = tile("queries%d" % a, [P, S2], U32)
+            for h in range(2):
+                nc.vector.tensor_copy(dst[:, HALF * h: HALF * (h + 1)],
+                                      query_tab[a][:].bitcast(U32).indirect(query_list[:, 16 * h: 16 * (h + 1)]))
+            return dst
+
+        def gather_keys(a):
+            dst = tile("keys%d" % a, [P, S], U32)
+            nc.vector.tensor_copy(dst[:].rearrange("p (b t m) -> p b m t", b=PASSES, t=PACK),
+                                  key_tab[a][:].bitcast(U32).indirect(key_list[:]))
+            return dst
+
+        key_sc_list = tile("key_sc_list", [P, S], U8)
+        key_sc = tile("key_sc", [P, S], U8)
+        query_sc = tile("query_sc", [P, S2], U8)
+        queries = [gather_queries(0)]
+        nc.vector.tensor_copy(key_sc_list[:], key_tab_sc[:].bitcast(U8).indirect(key_list[:]))
+        nc.vector.tensor_copy(key_sc[:].rearrange("p (b t m) -> p b t m", b=PASSES, t=PACK),
+                              key_sc_list[:].rearrange("p (b m t) -> p b t m", b=PASSES, t=PACK))
+        keys = [gather_keys(0)]
+        nc.vector.tensor_copy(query_sc[:], query_tab_sc[:].bitcast(U8).indirect(query_list[:]))
+        keys.append(gather_keys(1))
+        queries.append(gather_queries(1))
+
+        def score_pass(acc, h, u, a):
+            nc.tensor.matmul_mx(
+                out=acc[:],
+                lhsT=keys[a][:, P * u: P * (u + 1)].bitcast(FP8X4),
+                lhsT_scale=key_sc[4 * a:, P * u: P * (u + 1)],
+                rhs=queries[a][:, HALF * h: HALF * (h + 1)].bitcast(FP8X4),
+                rhs_scale=query_sc[8 + 4 * a:, HALF * h: HALF * (h + 1)],
+                start=(a == 0), stop=(a == PASSES - 1))
+
+        sig = {}
+        hb = {}
+        hq = {}
+        hs = {}
+        for h in range(2):
+            for b in range(PASSES):
+                sig[h, b] = tile("sig%d_%d" % (h, b), [P, PACK, HALF], F32)
+                hb[h, b] = tile("hb%d_%d" % (h, b), [P, HALF, PACK], BF16)
+                hq[h, b] = tile("hq%d_%d" % (h, b), [P, HALF], U32)
+                hs[h, b] = tile("hs%d_%d" % (h, b), [P, HALF], U8)
+
+        def weigh(h, b):
+            nc.vector.tensor_tensor(hb[h, b][:].rearrange("p (c i) t -> p c t i", i=4),
+                                    sig[h, b][:].rearrange("p t (c i) -> p c t i", i=4),
+                                    conf_sb[:, b, :].unsqueeze(1).unsqueeze(3).to_broadcast([P, HALF // 4, PACK, 4]), MULT)
+
+        def quant_h(h, b):
+            nc.vector.quantize_mx(out=hq[h, b][:].bitcast(FP8X4), scales=hs[h, b][:],
+                                  in_=hb[h, b][:].rearrange("p j t -> p (j t)"))
+
+        wb = {}
+        wq = {}
+        ws = {}
+
+        def cast_wg(c, b, on_vector):
+            wb[c, b] = tile("wb%d_%d" % (c, b), [P, WG_CHUNKS[c][1], PACK], BF16)
+            dst = wb[c, b][:].rearrange("p (c i) t -> p c t i", i=4)
+            src = wg_raw[c, b][:].rearrange("p t (c i) -> p c t i", i=4)
+            if on_vector:
+                nc.vector.tensor_copy(dst, src)
+            else:
+                nc.scalar.copy(dst, src)
+
+        def quant_wg(c, b):
+            wq[c, b] = tile("wq%d_%d" % (c, b), [P, WG_CHUNKS[c][1]], U32)
+            ws[c, b] = tile("ws%d_%d" % (c, b), [P, WG_CHUNKS[c][1]], U8)
+            nc.vector.quantize_mx(out=wq[c, b][:].bitcast(FP8X4), scales=ws[c, b][:],
+                                  in_=wb[c, b][:].rearrange("p n t -> p (n t)"))
+
+        def finish(h, n):
+            c = max(i for i in range(len(WG_CHUNKS)) if WG_CHUNKS[i][0] <= P * n)
+            m = n - WG_CHUNKS[c][0] // P
+            gate = psum.tile([P, HALF], F32, name="acc")
+            for b in range(PASSES):
+                nc.tensor.matmul_mx(
+                    out=gate[:],
+                    lhsT=wq[c, b][:, P * m: P * (m + 1)].bitcast(FP8X4),
+                    lhsT_scale=ws[c, b][:, P * m: P * (m + 1)],
+                    rhs=hq[h, b][:].bitcast(FP8X4), rhs_scale=hs[h, b][:],
+                    start=(b == 0), stop=(b == PASSES - 1))
+            ctxt = psum.tile([P, HALF], F32, name="acc")
+            for j0 in range(0, HALF, P):
+                for b in range(PASSES):
+                    nc.tensor.matmul_mx(
+                        out=ctxt[:, j0: j0 + P],
+                        lhsT=w4_w[:, b, 64 * n: 64 * (n + 1)].bitcast(U8).bitcast(FP4X4),
+                        lhsT_scale=w4_sc[:, b, 32 * n: 32 * (n + 1)].bitcast(U8),
+                        rhs=hq[h, b][:, j0: j0 + P].bitcast(FP8X4), rhs_scale=hs[h, b][:, j0: j0 + P],
+                        start=(b == 0), stop=(b == PASSES - 1))
+            gsig = tile("gsig%d_%d" % (h, n), [P, HALF], F32)
+            res = tile("res%d_%d" % (h, n), [P, HALF], F32)
+            nc.scalar.activation(gsig[:], gate[:], SIGMOID)
+            nc.vector.tensor_tensor(res[:], ctxt[:], gsig[:], MULT)
+            nc.sync.dma_start(out=out[P * n: P * (n + 1), HALF * h: HALF * (h + 1)], in_=res[:])
+
+        accs = [psum.tile([P, HALF], F32, name="acc") for u in range(8)]
+        for u in range(8):
+            score_pass(accs[u], 0, u, 0)
+        for u in range(8):
+            score_pass(accs[u], 0, u, 1)
+            nc.scalar.activation(sig[0, u // PACK][:, u % PACK, :], accs[u][:], SIGMOID)
+        for u in range(8):
+            acc = psum.tile([P, HALF], F32, name="acc")
+            for a in range(PASSES):
+                score_pass(acc, 1, u, a)
+            nc.scalar.activation(sig[1, u // PACK][:, u % PACK, :], acc[:], SIGMOID)
+        cast_wg(0, 0, True)
+        weigh(0, 0)
+        quant_wg(0, 0)
+        weigh(0, 1)
+        quant_h(0, 0)
+        cast_wg(0, 1, True)
+        quant_h(0, 1)
+        quant_wg(0, 1)
+        weigh(1, 0)
+        weigh(1, 1)
+        quant_h(1, 0)
+        quant_h(1, 1)
+        cast_wg(1, 0, False)
+        finish(0, 0)
+        finish(0, 1)
+        cast_wg(1, 1, False)
+        quant_wg(1, 0)
+        quant_wg(1, 1)
+        finish(1, 0)
+        finish(1, 1)
+        for c in (2, 3):
+            for b in range(PASSES):
+                cast_wg(c, b, False)
+        finish(0, 2)
+        finish(0, 3)
+        quant_wg(2, 0)
+        quant_wg(2, 1)
+        finish(1, 2)
+        finish(1, 3)
+        quant_wg(3, 0)
+        quant_wg(3, 1)
+        finish(0, 4)
+        finish(1, 4)
+        finish(0, 5)
+        finish(1, 5)

@@ -19,21 +19,27 @@ MULT = mybir.AluOpType.mult
 P = 128
 PACK = 4
 PASSES = 2
-QUADS = 4
-HALF = 256
+PASS_LEN = P * PACK
+BLOCKS = 16
+QUAD = 32
+QUAD_ROWS = 4
+SPREAD = P // (PASSES * BLOCKS)
+LIST_GROUP = 16
+BYTES_PER_I32 = 4
+HALF = S2 // 2
+RUN = 4
+BANKS = 8
+
 WG_CHUNKS = ((0, 256), (256, 256), (512, 128), (640, 128))
-SHARES = {
-    "keys0": "key_sc_list",
-    "keys1": "query_tab_sc",
-    "queries1": "key_tab1",
-    "wb0_0": "query_tab1",
-    "wb0_1": "sig0_0",
-    "wb1_0": "sig0_1",
-    "wb1_1": "hb0_0",
-    "wb2_0": "hb0_1",
-    "wb2_1": "sig1_0",
-    "wb3_0": "sig1_1",
-    "wb3_1": "hb1_0",
+
+REUSES = {
+    "wg_bf0_1": "h_bf0_1",
+    "wg_bf2_0": "h_bf0_1",
+    "wg_bf1_0": "att1_0",
+    "wg_bf2_1": "att1_0",
+    "wg_bf1_1": "att1_1",
+    "wg_bf3_0": "h_bf1_0",
+    "wg_bf3_1": "h_bf1_1",
 }
 
 
@@ -42,203 +48,237 @@ def tile_list_beam_sigmoid_glu_kernel(tc, tab_words, tab_scales, tab2_words, tab
     nc = tc.nc
     with ExitStack() as ctx:
         keep = ctx.enter_context(tc.tile_pool(name="keep", bufs=1))
-        psum = ctx.enter_context(tc.psum_pool(name="psum", bufs=8))
+        psum = ctx.enter_context(tc.psum_pool(name="psum", bufs=BANKS))
 
         def tile(name, shape, dtype):
-            return keep.tile(shape, dtype, name=name, tag=SHARES.get(name, name), align_bytes=64)
+            return keep.tile(shape, dtype, name=name, tag=REUSES.get(name, name), align_bytes=64)
 
-        key_list = keep.tile([P, S // 16], U16, name="key_list")
-        query_list = keep.tile([P, S2 // 16], U16, name="query_list")
-        key_tab = [tile("key_tab%d" % a, [P, T], I32) for a in range(PASSES)]
-        query_tab = [tile("query_tab%d" % a, [P, T2], I32) for a in range(PASSES)]
-        key_tab_sc = tile("key_tab_sc", [P, T // 4], I32)
-        query_tab_sc = tile("query_tab_sc", [P, T2 // 4], I32)
-        w4_sc = tile("w4_sc", [P, PASSES, N // 4], I32)
-        w4_w = tile("w4_w", [P, PASSES, N // 2], I32)
-        conf_sb = tile("conf_sb", [P, PASSES, PACK], F32)
+        def bank():
+            return psum.tile([P, 2 * HALF], F32, name="bank")
 
-        nc.vector.memset(key_tab_sc[:], 0)
-        nc.vector.memset(query_tab_sc[:], 0)
-        nc.vector.memset(w4_sc[:], 0)
+        key_list = keep.tile([P, S // LIST_GROUP], U16, name="key_list")
+        query_list = keep.tile([P, S2 // LIST_GROUP], U16, name="query_list")
+        key_table = [tile("key_table%d" % a, [P, T], I32) for a in range(PASSES)]
+        query_table = [tile("query_table%d" % a, [P, T2], I32) for a in range(PASSES)]
+        key_scale_table = tile("key_scale_table", [P, T // BYTES_PER_I32], I32)
+        query_scale_table = tile("query_scale_table", [P, T2 // BYTES_PER_I32], I32)
+        planes = [tile("planes%d" % a, [P, (S + S2) // BYTES_PER_I32], I32) for a in range(PASSES)]
+        w4 = tile("w4", [P, PASSES * (N // 2 + N // BYTES_PER_I32)], I32)
+        w4_codes = w4[:, :N].rearrange("p (b e) -> p b e", b=PASSES)
+        w4_planes = w4[:, N:].rearrange("p (b e) -> p b e", b=PASSES)
 
-        for q in range(QUADS):
-            nc.gpsimd.dma_start(out=key_tab_sc[32 * q: 32 * q + 8, :],
-                                in_=tab_scales[:, 4 * q: 4 * q + 4, :].bitcast(I32))
-        for q in range(QUADS):
-            nc.gpsimd.dma_start(out=query_tab_sc[32 * q + 8: 32 * q + 16, :],
-                                in_=tab2_scales[:, 4 * q: 4 * q + 4, :].bitcast(I32))
+        nc.vector.memset(key_scale_table[:], 0)
+        nc.gpsimd.memset(query_scale_table[:], 0)
+        for a in range(PASSES):
+            nc.vector.memset(planes[a][:], 0)
+        nc.gpsimd.memset(w4_planes, 0)
 
+        def load_words(dst, words, cols):
+            nc.sync.dma_start(out=dst[:, cols], in_=words.rearrange("p t i -> p (t i)").bitcast(I32)[:, cols])
+
+        def load_scale_rows(dst, scales):
+            nc.sync.dma_start(out=dst[0:P:SPREAD, :], in_=scales.rearrange("a q t -> (a q) t").bitcast(I32))
+
+        head = T // 4
         nc.sync.dma_start(query_list[:], offs2)
+        load_words(key_table[0], tab_words[0], slice(0, head))
         nc.sync.dma_start(key_list[:], offs)
+        load_scale_rows(query_scale_table, tab2_scales)
+        load_scale_rows(key_scale_table, tab_scales)
+        load_words(key_table[0], tab_words[0], slice(head, T))
+        load_words(key_table[1], tab_words[1], slice(0, T))
+        load_words(query_table[0], tab2_words[0], slice(0, T2))
 
-        def load_words(dst, words):
-            nc.sync.dma_start(out=dst[:], in_=words.rearrange("p t i -> p (t i)").bitcast(I32))
+        key_scales = tile("key_scales", [P, S], U8)
+        query_scales = tile("query_scales", [P, S2], U8)
+        scale_rows = tile("scale_rows", [P, (S + S2) // BYTES_PER_I32], I32)
+        nc.vector.tensor_copy(query_scales[:], query_scale_table[:].bitcast(U8).indirect(query_list[:]))
+        nc.vector.tensor_copy(key_scales[:], key_scale_table[:].bitcast(U8).indirect(key_list[:]))
+        nc.vector.tensor_copy(scale_rows[:, S // BYTES_PER_I32:], query_scales[:].bitcast(I32))
+        nc.vector.tensor_copy(scale_rows[:].bitcast(U8)[:, :S].rearrange("p (b t m) -> p b t m", b=PASSES, t=PACK),
+                              key_scales[:].rearrange("p (b m t) -> p b t m", b=PASSES, t=PACK))
 
-        load_words(query_tab[0], tab2_words[0])
-        load_words(key_tab[0], tab_words[0])
-        load_words(key_tab[1], tab_words[1])
-        load_words(query_tab[1], tab2_words[1])
+        def move_to_planes(a):
+            first = SPREAD * BLOCKS * a
+            for r in range(QUAD_ROWS):
+                nc.sync.dma_start(
+                    out=planes[a][r:P:QUAD, :],
+                    in_=scale_rows[first + SPREAD * r: first + SPREAD * BLOCKS: SPREAD * QUAD_ROWS, :])
 
-        wg_raw = {}
+        move_to_planes(0)
+        load_words(query_table[1], tab2_words[1], slice(0, T2))
+        move_to_planes(1)
+        conf_sb = tile("conf_sb", [P, PASSES, PACK], F32)
+        nc.sync.dma_start(out=conf_sb[:], in_=conf.rearrange("(b p t) -> p b t", b=PASSES, t=PACK))
+
+        keys = [tile("keys%d" % a, [P, S], U32) for a in range(PASSES)]
+        queries = [tile("queries%d" % a, [P, S2], U32) for a in range(PASSES)]
+        for a in range(PASSES):
+            nc.vector.tensor_copy(keys[a][:].rearrange("p (b t m) -> p b m t", b=PASSES, t=PACK),
+                                  key_table[a][:].bitcast(U32).indirect(key_list[:]))
+        list_cols = HALF // LIST_GROUP
+        for a in range(PASSES):
+            for h in range(2):
+                nc.vector.tensor_copy(
+                    queries[a][:, HALF * h: HALF * (h + 1)],
+                    query_table[a][:].bitcast(U32).indirect(query_list[:, list_cols * h: list_cols * (h + 1)]))
+
+        wg_f32 = {}
 
         def load_wg(c):
             n0, width = WG_CHUNKS[c]
             for b in range(PASSES):
-                wg_raw[c, b] = tile("wg_raw%d_%d" % (c, b), [P, PACK, width], F32)
-                nc.sync.dma_start(out=wg_raw[c, b][:],
-                                  in_=wg[512 * b: 512 * (b + 1), n0: n0 + width].rearrange("(p t) n -> p t n", t=PACK))
+                wg_f32[c, b] = tile("wg_f32_%d_%d" % (c, b), [P, PACK, width], F32)
+                rows = wg[PASS_LEN * b: PASS_LEN * (b + 1), n0: n0 + width]
+                nc.sync.dma_start(out=wg_f32[c, b][:], in_=rows.rearrange("(p t) n -> p t n", t=PACK))
 
-        nc.sync.dma_start(out=conf_sb[:], in_=conf.rearrange("(b p t) -> p b t", b=PASSES, t=PACK))
         load_wg(0)
-        nc.sync.dma_start(out=w4_w[:], in_=w4_words.rearrange("a p e -> p a e").bitcast(I32))
-        for q in range(QUADS):
-            nc.sync.dma_start(out=w4_sc[32 * q: 32 * q + 4, :, :],
-                              in_=w4_scales[:, 4 * q: 4 * q + 4, :].rearrange("a r n -> r a n").bitcast(I32))
+        nc.sync.dma_start(out=w4_codes, in_=w4_words.rearrange("b p e -> p b e").bitcast(I32))
+        for r in range(QUAD_ROWS):
+            nc.sync.dma_start(out=w4_planes[r:P:QUAD, :, :],
+                              in_=w4_scales[:, r:BLOCKS:QUAD_ROWS, :].rearrange("b q n -> q b n").bitcast(I32))
         for c in range(1, len(WG_CHUNKS)):
             load_wg(c)
 
-        def gather_queries(a):
-            dst = tile("queries%d" % a, [P, S2], U32)
-            for h in range(2):
-                nc.vector.tensor_copy(dst[:, HALF * h: HALF * (h + 1)],
-                                      query_tab[a][:].bitcast(U32).indirect(query_list[:, 16 * h: 16 * (h + 1)]))
-            return dst
-
-        def gather_keys(a):
-            dst = tile("keys%d" % a, [P, S], U32)
-            nc.vector.tensor_copy(dst[:].rearrange("p (b t m) -> p b m t", b=PASSES, t=PACK),
-                                  key_tab[a][:].bitcast(U32).indirect(key_list[:]))
-            return dst
-
-        key_sc_list = tile("key_sc_list", [P, S], U8)
-        key_sc = tile("key_sc", [P, S], U8)
-        query_sc = tile("query_sc", [P, S2], U8)
-        queries = [gather_queries(0)]
-        nc.vector.tensor_copy(key_sc_list[:], key_tab_sc[:].bitcast(U8).indirect(key_list[:]))
-        nc.vector.tensor_copy(key_sc[:].rearrange("p (b t m) -> p b t m", b=PASSES, t=PACK),
-                              key_sc_list[:].rearrange("p (b m t) -> p b t m", b=PASSES, t=PACK))
-        keys = [gather_keys(0)]
-        nc.vector.tensor_copy(query_sc[:], query_tab_sc[:].bitcast(U8).indirect(query_list[:]))
-        keys.append(gather_keys(1))
-        queries.append(gather_queries(1))
-
-        def score_pass(acc, h, u, a):
-            nc.tensor.matmul_mx(
-                out=acc[:],
-                lhsT=keys[a][:, P * u: P * (u + 1)].bitcast(FP8X4),
-                lhsT_scale=key_sc[4 * a:, P * u: P * (u + 1)],
-                rhs=queries[a][:, HALF * h: HALF * (h + 1)].bitcast(FP8X4),
-                rhs_scale=query_sc[8 + 4 * a:, HALF * h: HALF * (h + 1)],
-                start=(a == 0), stop=(a == PASSES - 1))
-
-        sig = {}
-        hb = {}
-        hq = {}
-        hs = {}
+        att = {}
+        h_bf = {}
         for h in range(2):
             for b in range(PASSES):
-                sig[h, b] = tile("sig%d_%d" % (h, b), [P, PACK, HALF], F32)
-                hb[h, b] = tile("hb%d_%d" % (h, b), [P, HALF, PACK], BF16)
-                hq[h, b] = tile("hq%d_%d" % (h, b), [P, HALF], U32)
-                hs[h, b] = tile("hs%d_%d" % (h, b), [P, HALF], U8)
+                att[h, b] = tile("att%d_%d" % (h, b), [P, PACK, HALF], F32)
+                h_bf[h, b] = tile("h_bf%d_%d" % (h, b), [P, HALF, PACK], BF16)
+        h_codes = [tile("h_codes%d" % b, [P, S2], U32) for b in range(PASSES)]
+        h_plane = [tile("h_plane%d" % b, [P, S2], U8) for b in range(PASSES)]
+        wg_bf = {}
+        wg_codes = {}
+        wg_plane = {}
+
+        def score_pass(acc, h, u, a):
+            plane = planes[a][:].bitcast(U8)
+            nc.tensor.matmul_mx(
+                out=acc,
+                lhsT=keys[a][:, P * u: P * (u + 1)].bitcast(FP8X4),
+                lhsT_scale=plane[:, P * u: P * (u + 1)],
+                rhs=queries[a][:, HALF * h: HALF * (h + 1)].bitcast(FP8X4),
+                rhs_scale=plane[:, S + HALF * h: S + HALF * (h + 1)],
+                start=(a == 0), stop=(a == PASSES - 1))
 
         def weigh(h, b):
-            nc.vector.tensor_tensor(hb[h, b][:].rearrange("p (c i) t -> p c t i", i=4),
-                                    sig[h, b][:].rearrange("p t (c i) -> p c t i", i=4),
-                                    conf_sb[:, b, :].unsqueeze(1).unsqueeze(3).to_broadcast([P, HALF // 4, PACK, 4]), MULT)
+            factor = conf_sb[:, b, :].unsqueeze(1).unsqueeze(3).to_broadcast([P, HALF // RUN, PACK, RUN])
+            nc.vector.tensor_tensor(h_bf[h, b][:].rearrange("p (x y) t -> p x t y", y=RUN),
+                                    att[h, b][:].rearrange("p t (x y) -> p x t y", y=RUN), factor, MULT)
 
-        def quant_h(h, b):
-            nc.vector.quantize_mx(out=hq[h, b][:].bitcast(FP8X4), scales=hs[h, b][:],
-                                  in_=hb[h, b][:].rearrange("p j t -> p (j t)"))
+        def quantise_h(h, b):
+            cols = slice(HALF * h, HALF * (h + 1))
+            nc.vector.quantize_mx(out=h_codes[b][:, cols].bitcast(FP8X4), scales=h_plane[b][:, cols],
+                                  in_=h_bf[h, b][:].rearrange("p j t -> p (j t)"))
 
-        wb = {}
-        wq = {}
-        ws = {}
+        def round_wg(c, b, copy):
+            wg_bf[c, b] = tile("wg_bf%d_%d" % (c, b), [P, WG_CHUNKS[c][1], PACK], BF16)
+            copy(wg_bf[c, b][:].rearrange("p (x y) t -> p x t y", y=RUN),
+                 wg_f32[c, b][:].rearrange("p t (x y) -> p x t y", y=RUN))
 
-        def cast_wg(c, b, on_vector):
-            wb[c, b] = tile("wb%d_%d" % (c, b), [P, WG_CHUNKS[c][1], PACK], BF16)
-            dst = wb[c, b][:].rearrange("p (c i) t -> p c t i", i=4)
-            src = wg_raw[c, b][:].rearrange("p t (c i) -> p c t i", i=4)
-            if on_vector:
-                nc.vector.tensor_copy(dst, src)
-            else:
-                nc.scalar.copy(dst, src)
+        def quantise_wg(c, b):
+            wg_codes[c, b] = tile("wg_codes%d_%d" % (c, b), [P, WG_CHUNKS[c][1]], U32)
+            wg_plane[c, b] = tile("wg_plane%d_%d" % (c, b), [P, WG_CHUNKS[c][1]], U8)
+            nc.vector.quantize_mx(out=wg_codes[c, b][:].bitcast(FP8X4), scales=wg_plane[c, b][:],
+                                  in_=wg_bf[c, b][:].rearrange("p n t -> p (n t)"))
 
-        def quant_wg(c, b):
-            wq[c, b] = tile("wq%d_%d" % (c, b), [P, WG_CHUNKS[c][1]], U32)
-            ws[c, b] = tile("ws%d_%d" % (c, b), [P, WG_CHUNKS[c][1]], U8)
-            nc.vector.quantize_mx(out=wq[c, b][:].bitcast(FP8X4), scales=ws[c, b][:],
-                                  in_=wb[c, b][:].rearrange("p n t -> p (n t)"))
-
-        def finish(h, n):
-            c = max(i for i in range(len(WG_CHUNKS)) if WG_CHUNKS[i][0] <= P * n)
-            m = n - WG_CHUNKS[c][0] // P
-            gate = psum.tile([P, HALF], F32, name="acc")
-            for b in range(PASSES):
-                nc.tensor.matmul_mx(
-                    out=gate[:],
-                    lhsT=wq[c, b][:, P * m: P * (m + 1)].bitcast(FP8X4),
-                    lhsT_scale=ws[c, b][:, P * m: P * (m + 1)],
-                    rhs=hq[h, b][:].bitcast(FP8X4), rhs_scale=hs[h, b][:],
-                    start=(b == 0), stop=(b == PASSES - 1))
-            ctxt = psum.tile([P, HALF], F32, name="acc")
-            for j0 in range(0, HALF, P):
+        def gate(h, pair):
+            acc = bank()
+            cols = slice(HALF * h, HALF * (h + 1))
+            for m in range(2):
+                n0 = P * (pair + m)
+                c = max(i for i in range(len(WG_CHUNKS)) if WG_CHUNKS[i][0] <= n0)
+                at = n0 - WG_CHUNKS[c][0]
                 for b in range(PASSES):
                     nc.tensor.matmul_mx(
-                        out=ctxt[:, j0: j0 + P],
-                        lhsT=w4_w[:, b, 64 * n: 64 * (n + 1)].bitcast(U8).bitcast(FP4X4),
-                        lhsT_scale=w4_sc[:, b, 32 * n: 32 * (n + 1)].bitcast(U8),
-                        rhs=hq[h, b][:, j0: j0 + P].bitcast(FP8X4), rhs_scale=hs[h, b][:, j0: j0 + P],
+                        out=acc[:, HALF * m: HALF * (m + 1)],
+                        lhsT=wg_codes[c, b][:, at: at + P].bitcast(FP8X4), lhsT_scale=wg_plane[c, b][:, at: at + P],
+                        rhs=h_codes[b][:, cols].bitcast(FP8X4), rhs_scale=h_plane[b][:, cols],
                         start=(b == 0), stop=(b == PASSES - 1))
-            gsig = tile("gsig%d_%d" % (h, n), [P, HALF], F32)
-            res = tile("res%d_%d" % (h, n), [P, HALF], F32)
-            nc.scalar.activation(gsig[:], gate[:], SIGMOID)
-            nc.vector.tensor_tensor(res[:], ctxt[:], gsig[:], MULT)
-            nc.sync.dma_start(out=out[P * n: P * (n + 1), HALF * h: HALF * (h + 1)], in_=res[:])
+            return acc
 
-        accs = [psum.tile([P, HALF], F32, name="acc") for u in range(8)]
-        for u in range(8):
-            score_pass(accs[u], 0, u, 0)
-        for u in range(8):
-            score_pass(accs[u], 0, u, 1)
-            nc.scalar.activation(sig[0, u // PACK][:, u % PACK, :], accs[u][:], SIGMOID)
-        for u in range(8):
-            acc = psum.tile([P, HALF], F32, name="acc")
-            for a in range(PASSES):
-                score_pass(acc, 1, u, a)
-            nc.scalar.activation(sig[1, u // PACK][:, u % PACK, :], acc[:], SIGMOID)
-        cast_wg(0, 0, True)
+        def context(h, pair):
+            acc = bank()
+            for m in range(2):
+                n0 = P * (pair + m)
+                for j in range(0, HALF, P):
+                    cols = slice(HALF * h + j, HALF * h + j + P)
+                    for b in range(PASSES):
+                        nc.tensor.matmul_mx(
+                            out=acc[:, HALF * m + j: HALF * m + j + P],
+                            lhsT=w4_codes[:, b, n0 // 2: (n0 + P) // 2].bitcast(U8).bitcast(FP4X4),
+                            lhsT_scale=w4_planes[:, b, n0 // BYTES_PER_I32: (n0 + P) // BYTES_PER_I32].bitcast(U8),
+                            rhs=h_codes[b][:, cols].bitcast(FP8X4), rhs_scale=h_plane[b][:, cols],
+                            start=(b == 0), stop=(b == PASSES - 1))
+            return acc
+
+        def finish(name, gate_sum, context_sum, dst):
+            gate_sig = tile("gate_sig" + name, [P, gate_sum.shape[1]], F32)
+            result = tile("result" + name, [P, gate_sum.shape[1]], F32)
+            nc.scalar.activation(gate_sig[:], gate_sum, SIGMOID)
+            nc.vector.tensor_tensor(result[:], context_sum, gate_sig[:], MULT)
+            nc.sync.dma_start(out=dst, in_=result[:].rearrange("p (m j) -> p m j", j=HALF))
+
+        def out_rows(h, pair):
+            return out[P * pair: P * (pair + 2), HALF * h: HALF * (h + 1)].rearrange("(m p) j -> p m j", m=2)
+
+        tiles_u = PASSES * PACK
+        accs = [bank() for u in range(tiles_u)]
+        for u in range(tiles_u):
+            score_pass(accs[u][:, :HALF], 0, u, 0)
+        for u in range(tiles_u):
+            score_pass(accs[u][:, :HALF], 0, u, 1)
+            nc.scalar.activation(att[0, u // PACK][:, u % PACK, :], accs[u][:, :HALF], SIGMOID)
+        for u in range(0, tiles_u, 2):
+            acc = bank()
+            for m in range(2):
+                for a in range(PASSES):
+                    score_pass(acc[:, HALF * m: HALF * (m + 1)], 1, u + m, a)
+            nc.scalar.activation(att[1, u // PACK][:, u % PACK: u % PACK + 2, :].rearrange("p t j -> p (t j)"),
+                                 acc[:], SIGMOID)
+
+        on_vector, on_scalar = nc.vector.tensor_copy, nc.scalar.copy
+        gates = {}
+        contexts = {}
+        round_wg(0, 0, on_vector)
         weigh(0, 0)
-        quant_wg(0, 0)
+        quantise_wg(0, 0)
         weigh(0, 1)
-        quant_h(0, 0)
-        cast_wg(0, 1, True)
-        quant_h(0, 1)
-        quant_wg(0, 1)
-        weigh(1, 0)
-        weigh(1, 1)
-        quant_h(1, 0)
-        quant_h(1, 1)
-        cast_wg(1, 0, False)
-        finish(0, 0)
-        finish(0, 1)
-        cast_wg(1, 1, False)
-        quant_wg(1, 0)
-        quant_wg(1, 1)
-        finish(1, 0)
-        finish(1, 1)
-        for c in (2, 3):
-            for b in range(PASSES):
-                cast_wg(c, b, False)
-        finish(0, 2)
-        finish(0, 3)
-        quant_wg(2, 0)
-        quant_wg(2, 1)
-        finish(1, 2)
-        finish(1, 3)
-        quant_wg(3, 0)
-        quant_wg(3, 1)
-        finish(0, 4)
-        finish(1, 4)
-        finish(0, 5)
-        finish(1, 5)
+        for b in range(PASSES):
+            quantise_h(0, b)
+        for pair in range(0, N // P, 2):
+            contexts[0, pair] = context(0, pair)
+        for b in range(PASSES):
+            weigh(1, b)
+        for b in range(PASSES):
+            quantise_h(1, b)
+        round_wg(0, 1, on_scalar)
+        for b in range(PASSES):
+            round_wg(1, b, on_scalar)
+
+        quantise_wg(0, 1)
+        gates[0, 0] = gate(0, 0)
+        contexts[1, 0] = context(1, 0)
+        gates[1, 0] = gate(1, 0)
+        for b in range(PASSES):
+            round_wg(2, b, on_vector)
+            quantise_wg(1, b)
+        gates[0, 2] = gate(0, 2)
+        contexts[1, 2] = context(1, 2)
+        for b in range(PASSES):
+            quantise_wg(2, b)
+        for h in range(2):
+            finish("%d_0" % h, gates[h, 0][:], contexts[h, 0][:], out_rows(h, 0))
+            round_wg(3, h, on_scalar)
+            quantise_wg(3, h)
+        gates[1, 2] = gate(1, 2)
+        contexts[1, 4] = context(1, 4)
+        for h in range(2):
+            gates[h, 4] = gate(h, 4)
+        for h in range(2):
+            finish("%d_2" % h, gates[h, 2][:], contexts[h, 2][:], out_rows(h, 2))
+        finish("0_4", gates[0, 4][:], contexts[0, 4][:], out_rows(0, 4))
+        for m in range(2):
+            cols = slice(HALF * m, HALF * (m + 1))
+            finish("1_4_%d" % m, gates[1, 4][:, cols], contexts[1, 4][:, cols], out_rows(1, 4)[:, m: m + 1, :])

@@ -27,20 +27,15 @@ SPREAD = P // (PASSES * BLOCKS)
 LIST_GROUP = 16
 BYTES_PER_I32 = 4
 HALF = S2 // 2
-RUN = 4
+RUN = 2
 BANKS = 8
 
-WG_CHUNKS = ((0, 256), (256, 256), (512, 128), (640, 128))
+WG_CHUNKS = ((0, 256), (256, 256), (512, 256))
+CHUNK = 256
+CHUNKS = N // CHUNK
+QUARTER = S2 // 4
 
-REUSES = {
-    "wg_bf0_1": "h_bf0_1",
-    "wg_bf2_0": "h_bf0_1",
-    "wg_bf1_0": "att1_0",
-    "wg_bf2_1": "att1_0",
-    "wg_bf1_1": "att1_1",
-    "wg_bf3_0": "h_bf1_0",
-    "wg_bf3_1": "h_bf1_1",
-}
+REUSES = {}
 
 
 def tile_list_beam_sigmoid_glu_kernel(tc, tab_words, tab_scales, tab2_words, tab2_scales,
@@ -48,13 +43,13 @@ def tile_list_beam_sigmoid_glu_kernel(tc, tab_words, tab_scales, tab2_words, tab
     nc = tc.nc
     with ExitStack() as ctx:
         keep = ctx.enter_context(tc.tile_pool(name="keep", bufs=1))
-        psum = ctx.enter_context(tc.psum_pool(name="psum", bufs=BANKS))
+        psum = ctx.enter_context(tc.psum_pool(name="psum", bufs=1))
 
         def tile(name, shape, dtype):
             return keep.tile(shape, dtype, name=name, tag=REUSES.get(name, name), align_bytes=64)
 
-        def bank():
-            return psum.tile([P, 2 * HALF], F32, name="bank")
+        def bank(number):
+            return psum.tile([P, 2 * HALF], F32, name="bank%d" % number)
 
         key_list = keep.tile([P, S // LIST_GROUP], U16, name="key_list")
         query_list = keep.tile([P, S2 // LIST_GROUP], U16, name="query_list")
@@ -141,75 +136,75 @@ def tile_list_beam_sigmoid_glu_kernel(tc, tab_words, tab_scales, tab2_words, tab
             load_wg(c)
 
         att = {}
-        h_bf = {}
         for h in range(2):
             for b in range(PASSES):
-                att[h, b] = tile("att%d_%d" % (h, b), [P, PACK, HALF], F32)
-                h_bf[h, b] = tile("h_bf%d_%d" % (h, b), [P, HALF, PACK], BF16)
-        h_codes = [tile("h_codes%d" % b, [P, S2], U32) for b in range(PASSES)]
-        h_plane = [tile("h_plane%d" % b, [P, S2], U8) for b in range(PASSES)]
-        wg_bf = {}
-        wg_codes = {}
-        wg_plane = {}
+                att[h, b] = tile("att%d_%d" % (h, b), [P, HALF, PACK], F32)
+        h_bf = [tile("h_bf%d" % h, [P, PASSES * HALF * PACK], BF16) for h in range(2)]
+        h_codes = [tile("h_codes%d" % h, [P, PASSES * HALF], U32) for h in range(2)]
+        h_plane = [tile("h_plane%d" % h, [P, PASSES * HALF], U8) for h in range(2)]
+        wg_bf = [tile("wg_bf%d" % c, [P, PASSES * CHUNK * PACK], BF16) for c in range(CHUNKS)]
+        wg_codes = [tile("wg_codes%d" % c, [P, PASSES * CHUNK], U32) for c in range(CHUNKS)]
+        wg_plane = [tile("wg_plane%d" % c, [P, PASSES * CHUNK], U8) for c in range(CHUNKS)]
 
-        def score_pass(acc, h, u, a):
+        def score_pass(acc, b, q, a):
             plane = planes[a][:].bitcast(U8)
-            nc.tensor.matmul_mx(
-                out=acc,
-                lhsT=keys[a][:, P * u: P * (u + 1)].bitcast(FP8X4),
-                lhsT_scale=plane[:, P * u: P * (u + 1)],
-                rhs=queries[a][:, HALF * h: HALF * (h + 1)].bitcast(FP8X4),
-                rhs_scale=plane[:, S + HALF * h: S + HALF * (h + 1)],
-                start=(a == 0), stop=(a == PASSES - 1))
+            for t in range(PACK):
+                u = PACK * b + t
+                nc.tensor.matmul_mx(
+                    out=acc[:, QUARTER * t: QUARTER * (t + 1)],
+                    lhsT=keys[a][:, P * u: P * (u + 1)].bitcast(FP8X4),
+                    lhsT_scale=plane[:, P * u: P * (u + 1)],
+                    rhs=queries[a][:, QUARTER * q: QUARTER * (q + 1)].bitcast(FP8X4),
+                    rhs_scale=plane[:, S + QUARTER * q: S + QUARTER * (q + 1)],
+                    start=(a == 0 and t == 0), stop=(a == PASSES - 1 and t == PACK - 1))
 
         def weigh(h, b):
-            factor = conf_sb[:, b, :].unsqueeze(1).unsqueeze(3).to_broadcast([P, HALF // RUN, PACK, RUN])
-            nc.vector.tensor_tensor(h_bf[h, b][:].rearrange("p (x y) t -> p x t y", y=RUN),
-                                    att[h, b][:].rearrange("p t (x y) -> p x t y", y=RUN), factor, MULT)
+            factor = conf_sb[:, b, :].unsqueeze(1).to_broadcast([P, HALF, PACK])
+            dst = h_bf[h][:, HALF * PACK * b: HALF * PACK * (b + 1)].rearrange("p (j t) -> p j t", t=PACK)
+            nc.vector.tensor_tensor(dst, att[h, b][:], factor, MULT)
 
-        def quantise_h(h, b):
-            cols = slice(HALF * h, HALF * (h + 1))
-            nc.vector.quantize_mx(out=h_codes[b][:, cols].bitcast(FP8X4), scales=h_plane[b][:, cols],
-                                  in_=h_bf[h, b][:].rearrange("p j t -> p (j t)"))
+        def quantise(codes, plane, rounded, first, last):
+            width = codes.shape[1] // PASSES
+            cols = slice(width * first, width * last)
+            nc.vector.quantize_mx(out=codes[:, cols].bitcast(FP8X4), scales=plane[:, cols],
+                                  in_=rounded[:, width * PACK * first: width * PACK * last])
+
+        def quantise_h(h, first=0, last=PASSES):
+            quantise(h_codes[h], h_plane[h], h_bf[h], first, last)
+
+        def quantise_wg(c, first=0, last=PASSES):
+            quantise(wg_codes[c], wg_plane[c], wg_bf[c], first, last)
 
         def round_wg(c, b, copy):
-            wg_bf[c, b] = tile("wg_bf%d_%d" % (c, b), [P, WG_CHUNKS[c][1], PACK], BF16)
-            copy(wg_bf[c, b][:].rearrange("p (x y) t -> p x t y", y=RUN),
+            dst = wg_bf[c][:, CHUNK * PACK * b: CHUNK * PACK * (b + 1)]
+            copy(dst.rearrange("p (x y t) -> p x t y", y=RUN, t=PACK),
                  wg_f32[c, b][:].rearrange("p t (x y) -> p x t y", y=RUN))
 
-        def quantise_wg(c, b):
-            wg_codes[c, b] = tile("wg_codes%d_%d" % (c, b), [P, WG_CHUNKS[c][1]], U32)
-            wg_plane[c, b] = tile("wg_plane%d_%d" % (c, b), [P, WG_CHUNKS[c][1]], U8)
-            nc.vector.quantize_mx(out=wg_codes[c, b][:].bitcast(FP8X4), scales=wg_plane[c, b][:],
-                                  in_=wg_bf[c, b][:].rearrange("p n t -> p (n t)"))
-
-        def gate(h, pair):
-            acc = bank()
-            cols = slice(HALF * h, HALF * (h + 1))
+        def gate(h, c, number):
+            acc = bank(number)
             for m in range(2):
-                n0 = P * (pair + m)
-                c = max(i for i in range(len(WG_CHUNKS)) if WG_CHUNKS[i][0] <= n0)
-                at = n0 - WG_CHUNKS[c][0]
                 for b in range(PASSES):
+                    cols = slice(CHUNK * b + P * m, CHUNK * b + P * (m + 1))
+                    picked = slice(HALF * b, HALF * (b + 1))
                     nc.tensor.matmul_mx(
                         out=acc[:, HALF * m: HALF * (m + 1)],
-                        lhsT=wg_codes[c, b][:, at: at + P].bitcast(FP8X4), lhsT_scale=wg_plane[c, b][:, at: at + P],
-                        rhs=h_codes[b][:, cols].bitcast(FP8X4), rhs_scale=h_plane[b][:, cols],
+                        lhsT=wg_codes[c][:, cols].bitcast(FP8X4), lhsT_scale=wg_plane[c][:, cols],
+                        rhs=h_codes[h][:, picked].bitcast(FP8X4), rhs_scale=h_plane[h][:, picked],
                         start=(b == 0), stop=(b == PASSES - 1))
             return acc
 
-        def context(h, pair):
-            acc = bank()
+        def context(h, c, number):
+            acc = bank(number)
             for m in range(2):
-                n0 = P * (pair + m)
+                n0 = CHUNK * c + P * m
                 for j in range(0, HALF, P):
-                    cols = slice(HALF * h + j, HALF * h + j + P)
                     for b in range(PASSES):
+                        picked = slice(HALF * b + j, HALF * b + j + P)
                         nc.tensor.matmul_mx(
                             out=acc[:, HALF * m + j: HALF * m + j + P],
                             lhsT=w4_codes[:, b, n0 // 2: (n0 + P) // 2].bitcast(U8).bitcast(FP4X4),
                             lhsT_scale=w4_planes[:, b, n0 // BYTES_PER_I32: (n0 + P) // BYTES_PER_I32].bitcast(U8),
-                            rhs=h_codes[b][:, cols].bitcast(FP8X4), rhs_scale=h_plane[b][:, cols],
+                            rhs=h_codes[h][:, picked].bitcast(FP8X4), rhs_scale=h_plane[h][:, picked],
                             start=(b == 0), stop=(b == PASSES - 1))
             return acc
 
@@ -220,65 +215,59 @@ def tile_list_beam_sigmoid_glu_kernel(tc, tab_words, tab_scales, tab2_words, tab
             nc.vector.tensor_tensor(result[:], context_sum, gate_sig[:], MULT)
             nc.sync.dma_start(out=dst, in_=result[:].rearrange("p (m j) -> p m j", j=HALF))
 
-        def out_rows(h, pair):
-            return out[P * pair: P * (pair + 2), HALF * h: HALF * (h + 1)].rearrange("(m p) j -> p m j", m=2)
+        def out_rows(h, c):
+            return out[CHUNK * c: CHUNK * (c + 1), HALF * h: HALF * (h + 1)].rearrange("(m p) j -> p m j", m=2)
 
-        tiles_u = PASSES * PACK
-        accs = [bank() for u in range(tiles_u)]
-        for u in range(tiles_u):
-            score_pass(accs[u][:, :HALF], 0, u, 0)
-        for u in range(tiles_u):
-            score_pass(accs[u][:, :HALF], 0, u, 1)
-            nc.scalar.activation(att[0, u // PACK][:, u % PACK, :], accs[u][:, :HALF], SIGMOID)
-        for u in range(0, tiles_u, 2):
-            acc = bank()
-            for m in range(2):
-                for a in range(PASSES):
-                    score_pass(acc[:, HALF * m: HALF * (m + 1)], 1, u + m, a)
-            nc.scalar.activation(att[1, u // PACK][:, u % PACK: u % PACK + 2, :].rearrange("p t j -> p (t j)"),
-                                 acc[:], SIGMOID)
+        for h in range(2):
+            order = [(b, 2 * h + x) for b in range(PASSES) for x in range(2)]
+            accs = [bank(number) for number in range(len(order))]
+            for number, (b, q) in enumerate(order):
+                score_pass(accs[number], b, q, 0)
+            for number, (b, q) in enumerate(order):
+                score_pass(accs[number], b, q, 1)
+                nc.scalar.activation(att[h, b][:, QUARTER * (q % 2): QUARTER * (q % 2 + 1), :],
+                                     accs[number][:].rearrange("p (t j) -> p j t", t=PACK), SIGMOID)
 
         on_vector, on_scalar = nc.vector.tensor_copy, nc.scalar.copy
         gates = {}
         contexts = {}
+
+        def finish_unit(h, c):
+            finish("%d_%d" % (h, c), gates[h, c][:], contexts[h, c][:], out_rows(h, c))
+
         round_wg(0, 0, on_vector)
-        weigh(0, 0)
-        quantise_wg(0, 0)
-        weigh(0, 1)
+        quantise_wg(0, 0, 1)
+        round_wg(0, 1, on_vector)
         for b in range(PASSES):
-            quantise_h(0, b)
-        for pair in range(0, N // P, 2):
-            contexts[0, pair] = context(0, pair)
+            weigh(0, b)
+        for b in range(PASSES):
+            quantise_h(0, b, b + 1)
+        for c in range(CHUNKS):
+            contexts[0, c] = context(0, c, 4 + c)
         for b in range(PASSES):
             weigh(1, b)
-        for b in range(PASSES):
-            quantise_h(1, b)
-        round_wg(0, 1, on_scalar)
-        for b in range(PASSES):
-            round_wg(1, b, on_scalar)
-
-        quantise_wg(0, 1)
-        gates[0, 0] = gate(0, 0)
-        contexts[1, 0] = context(1, 0)
-        gates[1, 0] = gate(1, 0)
-        for b in range(PASSES):
-            round_wg(2, b, on_vector)
-            quantise_wg(1, b)
-        gates[0, 2] = gate(0, 2)
-        contexts[1, 2] = context(1, 2)
-        for b in range(PASSES):
-            quantise_wg(2, b)
-        for h in range(2):
-            finish("%d_0" % h, gates[h, 0][:], contexts[h, 0][:], out_rows(h, 0))
-            round_wg(3, h, on_scalar)
-            quantise_wg(3, h)
-        gates[1, 2] = gate(1, 2)
-        contexts[1, 4] = context(1, 4)
-        for h in range(2):
-            gates[h, 4] = gate(h, 4)
-        for h in range(2):
-            finish("%d_2" % h, gates[h, 2][:], contexts[h, 2][:], out_rows(h, 2))
-        finish("0_4", gates[0, 4][:], contexts[0, 4][:], out_rows(0, 4))
+        quantise_wg(0, 1, 2)
+        quantise_h(1)
+        gates[0, 0] = gate(0, 0, 0)
+        contexts[1, 0] = context(1, 0, 1)
+        gates[1, 0] = gate(1, 0, 2)
+        round_wg(1, 0, on_scalar)
+        round_wg(1, 1, on_scalar)
+        round_wg(2, 0, on_scalar)
+        quantise_wg(1)
+        gates[0, 1] = gate(0, 1, 3)
+        gates[1, 1] = gate(1, 1, 7)
+        round_wg(2, 1, on_vector)
+        finish_unit(0, 0)
+        contexts[1, 1] = context(1, 1, 0)
+        quantise_wg(2)
+        finish_unit(1, 0)
+        gates[0, 2] = gate(0, 2, 2)
+        finish_unit(0, 1)
+        gates[1, 2] = gate(1, 2, 3)
+        contexts[1, 2] = context(1, 2, 4)
+        finish_unit(1, 1)
+        finish_unit(0, 2)
         for m in range(2):
             cols = slice(HALF * m, HALF * (m + 1))
-            finish("1_4_%d" % m, gates[1, 4][:, cols], contexts[1, 4][:, cols], out_rows(1, 4)[:, m: m + 1, :])
+            finish("1_2_%d" % m, gates[1, 2][:, cols], contexts[1, 2][:, cols], out_rows(1, 2)[:, m: m + 1, :])

@@ -82,7 +82,6 @@ def tile_list_beam_sigmoid_glu_kernel(tc, tab_words, tab_scales, tab2_words, tab
         load_scale_rows(key_scale_table, tab_scales)
         load_words(key_table[0], tab_words[0], slice(head, T))
         load_words(key_table[1], tab_words[1], slice(0, T))
-        load_words(query_table[0], tab2_words[0], slice(0, T2))
 
         key_scales = tile("key_scales", [P, S], U8)
         query_scales = tile("query_scales", [P, S2], U8)
@@ -97,12 +96,12 @@ def tile_list_beam_sigmoid_glu_kernel(tc, tab_words, tab_scales, tab2_words, tab
             first = SPREAD * BLOCKS * a
             for r in range(QUAD_ROWS):
                 nc.sync.dma_start(
-                    out=planes[a][r:P:QUAD, :],
+                    out=planes[a][QUAD_ROWS * a + r:P:QUAD, :],
                     in_=scale_rows[first + SPREAD * r: first + SPREAD * BLOCKS: SPREAD * QUAD_ROWS, :])
 
-        move_to_planes(0)
-        load_words(query_table[1], tab2_words[1], slice(0, T2))
-        move_to_planes(1)
+        for a in range(PASSES):
+            move_to_planes(a)
+            load_words(query_table[a], tab2_words[a], slice(0, T2))
         conf_sb = tile("conf_sb", [P, PASSES, PACK], F32)
         nc.sync.dma_start(out=conf_sb[:], in_=conf.rearrange("(b p t) -> p b t", b=PASSES, t=PACK))
 
@@ -147,7 +146,7 @@ def tile_list_beam_sigmoid_glu_kernel(tc, tab_words, tab_scales, tab2_words, tab
         wg_plane = [tile("wg_plane%d" % c, [P, PASSES * CHUNK], U8) for c in range(CHUNKS)]
 
         def score_pass(acc, b, q, a):
-            plane = planes[a][:].bitcast(U8)
+            plane = planes[a][QUAD_ROWS * a:, :].bitcast(U8)
             for t in range(PACK):
                 u = PACK * b + t
                 nc.tensor.matmul_mx(

@@ -31,6 +31,7 @@ RUN = 2
 BANKS = 8
 
 WG_CHUNKS = ((0, 256), (256, 256), (512, 256))
+SCORE_BANKS = 3
 CHUNK = 256
 CHUNKS = N // CHUNK
 QUARTER = S2 // 4
@@ -75,8 +76,8 @@ def tile_list_beam_sigmoid_glu_kernel(tc, tab_words, tab_scales, tab2_words, tab
             nc.sync.dma_start(out=dst[0:P:SPREAD, :], in_=scales.rearrange("a q t -> (a q) t").bitcast(I32))
 
         head = T // 4
-        nc.sync.dma_start(query_list[:], offs2)
         load_words(key_table[0], tab_words[0], slice(0, head))
+        nc.sync.dma_start(query_list[:], offs2)
         nc.sync.dma_start(key_list[:], offs)
         load_scale_rows(query_scale_table, tab2_scales)
         load_scale_rows(key_scale_table, tab_scales)
@@ -102,8 +103,6 @@ def tile_list_beam_sigmoid_glu_kernel(tc, tab_words, tab_scales, tab2_words, tab
         for a in range(PASSES):
             move_to_planes(a)
             load_words(query_table[a], tab2_words[a], slice(0, T2))
-        conf_sb = tile("conf_sb", [P, PASSES, PACK], F32)
-        nc.sync.dma_start(out=conf_sb[:], in_=conf.rearrange("(b p t) -> p b t", b=PASSES, t=PACK))
 
         keys = [tile("keys%d" % a, [P, S], U32) for a in range(PASSES)]
         queries = [tile("queries%d" % a, [P, S2], U32) for a in range(PASSES)]
@@ -126,6 +125,8 @@ def tile_list_beam_sigmoid_glu_kernel(tc, tab_words, tab_scales, tab2_words, tab
                 rows = wg[PASS_LEN * b: PASS_LEN * (b + 1), n0: n0 + width]
                 nc.sync.dma_start(out=wg_f32[c, b][:], in_=rows.rearrange("(p t) n -> p t n", t=PACK))
 
+        conf_sb = tile("conf_sb", [P, PASSES, PACK], F32)
+        nc.sync.dma_start(out=conf_sb[:], in_=conf.rearrange("(b p t) -> p b t", b=PASSES, t=PACK))
         load_wg(0)
         nc.sync.dma_start(out=w4_codes, in_=w4_words.rearrange("b p e -> p b e").bitcast(I32))
         for r in range(QUAD_ROWS):
@@ -217,15 +218,13 @@ def tile_list_beam_sigmoid_glu_kernel(tc, tab_words, tab_scales, tab2_words, tab
         def out_rows(h, c):
             return out[CHUNK * c: CHUNK * (c + 1), HALF * h: HALF * (h + 1)].rearrange("(m p) j -> p m j", m=2)
 
-        for h in range(2):
-            order = [(b, 2 * h + x) for b in range(PASSES) for x in range(2)]
-            accs = [bank(number) for number in range(len(order))]
-            for number, (b, q) in enumerate(order):
-                score_pass(accs[number], b, q, 0)
-            for number, (b, q) in enumerate(order):
-                score_pass(accs[number], b, q, 1)
-                nc.scalar.activation(att[h, b][:, QUARTER * (q % 2): QUARTER * (q % 2 + 1), :],
-                                     accs[number][:].rearrange("p (t j) -> p j t", t=PACK), SIGMOID)
+        order = [(h, b, x) for h in range(2) for b in range(PASSES) for x in range(2)]
+        for number, (h, b, x) in enumerate(order):
+            acc = bank(number % SCORE_BANKS)
+            for a in range(PASSES):
+                score_pass(acc, b, 2 * h + x, a)
+            nc.scalar.activation(att[h, b][:, QUARTER * x: QUARTER * (x + 1), :],
+                                 acc[:].rearrange("p (t j) -> p j t", t=PACK), SIGMOID)
 
         on_vector, on_scalar = nc.vector.tensor_copy, nc.scalar.copy
         gates = {}
@@ -242,29 +241,29 @@ def tile_list_beam_sigmoid_glu_kernel(tc, tab_words, tab_scales, tab2_words, tab
         for b in range(PASSES):
             quantise_h(0, b, b + 1)
         for c in range(CHUNKS):
-            contexts[0, c] = context(0, c, 4 + c)
+            contexts[0, c] = context(0, c, 3 + c)
         for b in range(PASSES):
             weigh(1, b)
         quantise_wg(0, 1, 2)
         quantise_h(1)
-        gates[0, 0] = gate(0, 0, 0)
-        contexts[1, 0] = context(1, 0, 1)
+        gates[0, 0] = gate(0, 0, 6)
+        contexts[1, 0] = context(1, 0, 7)
         gates[1, 0] = gate(1, 0, 2)
         round_wg(1, 0, on_scalar)
         round_wg(1, 1, on_scalar)
         round_wg(2, 0, on_scalar)
         quantise_wg(1)
-        gates[0, 1] = gate(0, 1, 3)
-        gates[1, 1] = gate(1, 1, 7)
+        gates[0, 1] = gate(0, 1, 0)
+        gates[1, 1] = gate(1, 1, 1)
         round_wg(2, 1, on_vector)
         finish_unit(0, 0)
-        contexts[1, 1] = context(1, 1, 0)
+        contexts[1, 1] = context(1, 1, 6)
         quantise_wg(2)
         finish_unit(1, 0)
         gates[0, 2] = gate(0, 2, 2)
         finish_unit(0, 1)
-        gates[1, 2] = gate(1, 2, 3)
-        contexts[1, 2] = context(1, 2, 4)
+        gates[1, 2] = gate(1, 2, 0)
+        contexts[1, 2] = context(1, 2, 3)
         finish_unit(1, 1)
         finish_unit(0, 2)
         for m in range(2):

@@ -36,7 +36,7 @@ CHUNK = 256
 CHUNKS = N // CHUNK
 QUARTER = S2 // 4
 
-REUSES = {}
+REUSES = {"wg_bf1": "att0_1", "wg_bf2": "att1_0"}
 
 
 def tile_list_beam_sigmoid_glu_kernel(tc, tab_words, tab_scales, tab2_words, tab2_scales,
@@ -96,7 +96,7 @@ def tile_list_beam_sigmoid_glu_kernel(tc, tab_words, tab_scales, tab2_words, tab
         def move_to_planes(a):
             first = SPREAD * BLOCKS * a
             for r in range(QUAD_ROWS):
-                nc.sync.dma_start(
+                (nc.sync, nc.gpsimd)[a].dma_start(
                     out=planes[a][QUAD_ROWS * a + r:P:QUAD, :],
                     in_=scale_rows[first + SPREAD * r: first + SPREAD * BLOCKS: SPREAD * QUAD_ROWS, :])
 

@@ -26,15 +26,15 @@ QUAD_ROWS = 4
 SPREAD = P // (PASSES * BLOCKS)
 LIST_GROUP = 16
 BYTES_PER_I32 = 4
-HALF = S2 // 2
+HALVES = 2
+HALF = S2 // HALVES
+QUARTER = HALF // 2
 RUN = 2
 BANKS = 8
-
-WG_CHUNKS = ((0, 256), (256, 256), (512, 256))
 SCORE_BANKS = 3
-CHUNK = 256
+CHUNK = 2 * P
 CHUNKS = N // CHUNK
-QUARTER = S2 // 4
+KEY_HEAD = T // 4
 
 REUSES = {"wg_bf1": "att0_1", "wg_bf2": "att1_0"}
 
@@ -75,13 +75,12 @@ def tile_list_beam_sigmoid_glu_kernel(tc, tab_words, tab_scales, tab2_words, tab
         def load_scale_rows(dst, scales):
             nc.sync.dma_start(out=dst[0:P:SPREAD, :], in_=scales.rearrange("a q t -> (a q) t").bitcast(I32))
 
-        head = T // 4
-        load_words(key_table[0], tab_words[0], slice(0, head))
+        load_words(key_table[0], tab_words[0], slice(0, KEY_HEAD))
         nc.sync.dma_start(query_list[:], offs2)
         nc.sync.dma_start(key_list[:], offs)
         load_scale_rows(query_scale_table, tab2_scales)
         load_scale_rows(key_scale_table, tab_scales)
-        load_words(key_table[0], tab_words[0], slice(head, T))
+        load_words(key_table[0], tab_words[0], slice(KEY_HEAD, T))
         load_words(key_table[1], tab_words[1], slice(0, T))
 
         key_scales = tile("key_scales", [P, S], U8)
@@ -93,15 +92,15 @@ def tile_list_beam_sigmoid_glu_kernel(tc, tab_words, tab_scales, tab2_words, tab
         nc.vector.tensor_copy(scale_rows[:].bitcast(U8)[:, :S].rearrange("p (b t m) -> p b t m", b=PASSES, t=PACK),
                               key_scales[:].rearrange("p (b m t) -> p b t m", b=PASSES, t=PACK))
 
-        def move_to_planes(a):
+        def move_to_planes(a, queue):
             first = SPREAD * BLOCKS * a
             for r in range(QUAD_ROWS):
-                (nc.sync, nc.gpsimd)[a].dma_start(
+                queue.dma_start(
                     out=planes[a][QUAD_ROWS * a + r:P:QUAD, :],
                     in_=scale_rows[first + SPREAD * r: first + SPREAD * BLOCKS: SPREAD * QUAD_ROWS, :])
 
-        for a in range(PASSES):
-            move_to_planes(a)
+        for a, queue in enumerate((nc.sync, nc.gpsimd)):
+            move_to_planes(a, queue)
             load_words(query_table[a], tab2_words[a], slice(0, T2))
 
         keys = [tile("keys%d" % a, [P, S], U32) for a in range(PASSES)]
@@ -111,7 +110,7 @@ def tile_list_beam_sigmoid_glu_kernel(tc, tab_words, tab_scales, tab2_words, tab
                                   key_table[a][:].bitcast(U32).indirect(key_list[:]))
         list_cols = HALF // LIST_GROUP
         for a in range(PASSES):
-            for h in range(2):
+            for h in range(HALVES):
                 nc.vector.tensor_copy(
                     queries[a][:, HALF * h: HALF * (h + 1)],
                     query_table[a][:].bitcast(U32).indirect(query_list[:, list_cols * h: list_cols * (h + 1)]))
@@ -119,10 +118,9 @@ def tile_list_beam_sigmoid_glu_kernel(tc, tab_words, tab_scales, tab2_words, tab
         wg_f32 = {}
 
         def load_wg(c):
-            n0, width = WG_CHUNKS[c]
             for b in range(PASSES):
-                wg_f32[c, b] = tile("wg_f32_%d_%d" % (c, b), [P, PACK, width], F32)
-                rows = wg[PASS_LEN * b: PASS_LEN * (b + 1), n0: n0 + width]
+                wg_f32[c, b] = tile("wg_f32_%d_%d" % (c, b), [P, PACK, CHUNK], F32)
+                rows = wg[PASS_LEN * b: PASS_LEN * (b + 1), CHUNK * c: CHUNK * (c + 1)]
                 nc.sync.dma_start(out=wg_f32[c, b][:], in_=rows.rearrange("(p t) n -> p t n", t=PACK))
 
         conf_sb = tile("conf_sb", [P, PASSES, PACK], F32)
@@ -132,21 +130,21 @@ def tile_list_beam_sigmoid_glu_kernel(tc, tab_words, tab_scales, tab2_words, tab
         for r in range(QUAD_ROWS):
             nc.sync.dma_start(out=w4_planes[r:P:QUAD, :, :],
                               in_=w4_scales[:, r:BLOCKS:QUAD_ROWS, :].rearrange("b q n -> q b n").bitcast(I32))
-        for c in range(1, len(WG_CHUNKS)):
+        for c in range(1, CHUNKS):
             load_wg(c)
 
         att = {}
-        for h in range(2):
+        for h in range(HALVES):
             for b in range(PASSES):
                 att[h, b] = tile("att%d_%d" % (h, b), [P, HALF, PACK], F32)
-        h_bf = [tile("h_bf%d" % h, [P, PASSES * HALF * PACK], BF16) for h in range(2)]
-        h_codes = [tile("h_codes%d" % h, [P, PASSES * HALF], U32) for h in range(2)]
-        h_plane = [tile("h_plane%d" % h, [P, PASSES * HALF], U8) for h in range(2)]
+        h_bf = [tile("h_bf%d" % h, [P, PASSES * HALF * PACK], BF16) for h in range(HALVES)]
+        h_codes = [tile("h_codes%d" % h, [P, PASSES * HALF], U32) for h in range(HALVES)]
+        h_plane = [tile("h_plane%d" % h, [P, PASSES * HALF], U8) for h in range(HALVES)]
         wg_bf = [tile("wg_bf%d" % c, [P, PASSES * CHUNK * PACK], BF16) for c in range(CHUNKS)]
         wg_codes = [tile("wg_codes%d" % c, [P, PASSES * CHUNK], U32) for c in range(CHUNKS)]
         wg_plane = [tile("wg_plane%d" % c, [P, PASSES * CHUNK], U8) for c in range(CHUNKS)]
 
-        def score_pass(acc, b, q, a):
+        def score_pass(acc, b, quarter, a):
             plane = planes[a][QUAD_ROWS * a:, :].bitcast(U8)
             for t in range(PACK):
                 u = PACK * b + t
@@ -154,8 +152,8 @@ def tile_list_beam_sigmoid_glu_kernel(tc, tab_words, tab_scales, tab2_words, tab
                     out=acc[:, QUARTER * t: QUARTER * (t + 1)],
                     lhsT=keys[a][:, P * u: P * (u + 1)].bitcast(FP8X4),
                     lhsT_scale=plane[:, P * u: P * (u + 1)],
-                    rhs=queries[a][:, QUARTER * q: QUARTER * (q + 1)].bitcast(FP8X4),
-                    rhs_scale=plane[:, S + QUARTER * q: S + QUARTER * (q + 1)],
+                    rhs=queries[a][:, QUARTER * quarter: QUARTER * (quarter + 1)].bitcast(FP8X4),
+                    rhs_scale=plane[:, S + QUARTER * quarter: S + QUARTER * (quarter + 1)],
                     start=(a == 0 and t == 0), stop=(a == PASSES - 1 and t == PACK - 1))
 
         def weigh(h, b):
@@ -169,8 +167,11 @@ def tile_list_beam_sigmoid_glu_kernel(tc, tab_words, tab_scales, tab2_words, tab
             nc.vector.quantize_mx(out=codes[:, cols].bitcast(FP8X4), scales=plane[:, cols],
                                   in_=rounded[:, width * PACK * first: width * PACK * last])
 
-        def quantise_h(h, first=0, last=PASSES):
-            quantise(h_codes[h], h_plane[h], h_bf[h], first, last)
+        def make_h(h):
+            for b in range(PASSES):
+                weigh(h, b)
+            for b in range(PASSES):
+                quantise(h_codes[h], h_plane[h], h_bf[h], b, b + 1)
 
         def quantise_wg(c, first=0, last=PASSES):
             quantise(wg_codes[c], wg_plane[c], wg_bf[c], first, last)
@@ -180,9 +181,8 @@ def tile_list_beam_sigmoid_glu_kernel(tc, tab_words, tab_scales, tab2_words, tab
             copy(dst.rearrange("p (x y t) -> p x t y", y=RUN, t=PACK),
                  wg_f32[c, b][:].rearrange("p t (x y) -> p x t y", y=RUN))
 
-        def gate(h, c, number):
-            acc = bank(number)
-            for m in range(2):
+        def gate(h, c, acc):
+            for m in range(CHUNK // P):
                 for b in range(PASSES):
                     cols = slice(CHUNK * b + P * m, CHUNK * b + P * (m + 1))
                     picked = slice(HALF * b, HALF * (b + 1))
@@ -191,11 +191,9 @@ def tile_list_beam_sigmoid_glu_kernel(tc, tab_words, tab_scales, tab2_words, tab
                         lhsT=wg_codes[c][:, cols].bitcast(FP8X4), lhsT_scale=wg_plane[c][:, cols],
                         rhs=h_codes[h][:, picked].bitcast(FP8X4), rhs_scale=h_plane[h][:, picked],
                         start=(b == 0), stop=(b == PASSES - 1))
-            return acc
 
-        def context(h, c, number):
-            acc = bank(number)
-            for m in range(2):
+        def context(h, c, acc):
+            for m in range(CHUNK // P):
                 n0 = CHUNK * c + P * m
                 for j in range(0, HALF, P):
                     for b in range(PASSES):
@@ -206,7 +204,6 @@ def tile_list_beam_sigmoid_glu_kernel(tc, tab_words, tab_scales, tab2_words, tab
                             lhsT_scale=w4_planes[:, b, n0 // BYTES_PER_I32: (n0 + P) // BYTES_PER_I32].bitcast(U8),
                             rhs=h_codes[h][:, picked].bitcast(FP8X4), rhs_scale=h_plane[h][:, picked],
                             start=(b == 0), stop=(b == PASSES - 1))
-            return acc
 
         def finish(name, gate_sum, context_sum, dst):
             gate_sig = tile("gate_sig" + name, [P, gate_sum.shape[1]], F32)
@@ -216,56 +213,55 @@ def tile_list_beam_sigmoid_glu_kernel(tc, tab_words, tab_scales, tab2_words, tab
             nc.sync.dma_start(out=dst, in_=result[:].rearrange("p (m j) -> p m j", j=HALF))
 
         def out_rows(h, c):
-            return out[CHUNK * c: CHUNK * (c + 1), HALF * h: HALF * (h + 1)].rearrange("(m p) j -> p m j", m=2)
+            return out[CHUNK * c: CHUNK * (c + 1), HALF * h: HALF * (h + 1)].rearrange("(m p) j -> p m j", p=P)
 
-        order = [(h, b, x) for h in range(2) for b in range(PASSES) for x in range(2)]
-        for number, (h, b, x) in enumerate(order):
+        scores = [(h, b, x) for h in range(HALVES) for b in range(PASSES) for x in range(HALF // QUARTER)]
+        for number, (h, b, x) in enumerate(scores):
             acc = bank(number % SCORE_BANKS)
             for a in range(PASSES):
-                score_pass(acc, b, 2 * h + x, a)
+                score_pass(acc, b, HALF // QUARTER * h + x, a)
             nc.scalar.activation(att[h, b][:, QUARTER * x: QUARTER * (x + 1), :],
                                  acc[:].rearrange("p (t j) -> p j t", t=PACK), SIGMOID)
 
+        free = list(range(SCORE_BANKS, BANKS))
+        free.extend(number % SCORE_BANKS for number in range(len(scores) - SCORE_BANKS, len(scores)))
+        waiting = [(h, c) for c in range(CHUNKS) for h in range(HALVES)]
+        sums = {}
+
+        def finish_oldest():
+            h, c = waiting.pop(0)
+            finish("%d_%d" % (h, c), sums[gate, h, c][1][:], sums[context, h, c][1][:], out_rows(h, c))
+            free.extend((sums[gate, h, c][0], sums[context, h, c][0]))
+
+        def multiply(step, h, c):
+            if not free:
+                finish_oldest()
+            number = free.pop(0)
+            sums[step, h, c] = (number, bank(number))
+            step(h, c, sums[step, h, c][1])
+
         on_vector, on_scalar = nc.vector.tensor_copy, nc.scalar.copy
-        gates = {}
-        contexts = {}
-
-        def finish_unit(h, c):
-            finish("%d_%d" % (h, c), gates[h, c][:], contexts[h, c][:], out_rows(h, c))
-
         round_wg(0, 0, on_vector)
         quantise_wg(0, 0, 1)
         round_wg(0, 1, on_vector)
-        for b in range(PASSES):
-            weigh(0, b)
-        for b in range(PASSES):
-            quantise_h(0, b, b + 1)
+        make_h(0)
         for c in range(CHUNKS):
-            contexts[0, c] = context(0, c, 3 + c)
-        for b in range(PASSES):
-            weigh(1, b)
-        quantise_wg(0, 1, 2)
-        quantise_h(1)
-        gates[0, 0] = gate(0, 0, 6)
-        contexts[1, 0] = context(1, 0, 7)
-        gates[1, 0] = gate(1, 0, 2)
-        round_wg(1, 0, on_scalar)
-        round_wg(1, 1, on_scalar)
-        round_wg(2, 0, on_scalar)
-        quantise_wg(1)
-        gates[0, 1] = gate(0, 1, 0)
-        gates[1, 1] = gate(1, 1, 1)
-        round_wg(2, 1, on_vector)
-        finish_unit(0, 0)
-        contexts[1, 1] = context(1, 1, 6)
-        quantise_wg(2)
-        finish_unit(1, 0)
-        gates[0, 2] = gate(0, 2, 2)
-        finish_unit(0, 1)
-        gates[1, 2] = gate(1, 2, 0)
-        contexts[1, 2] = context(1, 2, 3)
-        finish_unit(1, 1)
-        finish_unit(0, 2)
-        for m in range(2):
+            multiply(context, 0, c)
+        make_h(1)
+        quantise_wg(0, 1, PASSES)
+
+        for c in range(CHUNKS):
+            if c > 0:
+                round_wg(c, 0, on_scalar)
+                round_wg(c, 1, on_vector if c == CHUNKS - 1 else on_scalar)
+                quantise_wg(c)
+            for h in range(HALVES):
+                multiply(gate, h, c)
+            multiply(context, 1, c)
+        for unit in range(len(waiting) - 1):
+            finish_oldest()
+        h, c = waiting.pop(0)
+        for m in range(CHUNK // P):
             cols = slice(HALF * m, HALF * (m + 1))
-            finish("1_2_%d" % m, gates[1, 2][:, cols], contexts[1, 2][:, cols], out_rows(1, 2)[:, m: m + 1, :])
+            finish("%d_%d_%d" % (h, c, m), sums[gate, h, c][1][:, cols], sums[context, h, c][1][:, cols],
+                   out_rows(h, c)[:, m: m + 1, :])

@@ -23,7 +23,7 @@ PASS_LEN = P * PACK
 BLOCKS = 16
 QUAD = 32
 QUAD_ROWS = 4
-SPREAD = P // (PASSES * BLOCKS)
+SCALE_ROWS = PASSES * BLOCKS
 LIST_GROUP = 16
 BYTES_PER_I32 = 4
 HALVES = 2
@@ -34,7 +34,6 @@ BANKS = 8
 SCORE_BANKS = 3
 CHUNK = 2 * P
 CHUNKS = N // CHUNK
-KEY_HEAD = T // 4
 
 REUSES = {"wg_bf1": "att0_1", "wg_bf2": "att1_0"}
 
@@ -63,8 +62,9 @@ def tile_list_beam_sigmoid_glu_kernel(tc, tab_words, tab_scales, tab2_words, tab
         w4_codes = w4[:, :N].rearrange("p (b e) -> p b e", b=PASSES)
         w4_planes = w4[:, N:].rearrange("p (b e) -> p b e", b=PASSES)
 
-        nc.vector.memset(key_scale_table[:], 0)
-        nc.gpsimd.memset(query_scale_table[:], 0)
+        for rows in (slice(QUAD, 2 * QUAD), slice(2 * QUAD, P)):
+            nc.vector.memset(key_scale_table[rows, :], 0)
+            nc.gpsimd.memset(query_scale_table[rows, :], 0)
         for a in range(PASSES):
             nc.vector.memset(planes[a][:], 0)
         nc.gpsimd.memset(w4_planes, 0)
@@ -73,34 +73,33 @@ def tile_list_beam_sigmoid_glu_kernel(tc, tab_words, tab_scales, tab2_words, tab
             nc.sync.dma_start(out=dst[:, cols], in_=words.rearrange("p t i -> p (t i)").bitcast(I32)[:, cols])
 
         def load_scale_rows(dst, scales):
-            nc.sync.dma_start(out=dst[0:P:SPREAD, :], in_=scales.rearrange("a q t -> (a q) t").bitcast(I32))
+            nc.sync.dma_start(out=dst[:SCALE_ROWS, :], in_=scales.rearrange("a q t -> (a q) t").bitcast(I32))
 
-        load_words(key_table[0], tab_words[0], slice(0, KEY_HEAD))
-        nc.sync.dma_start(query_list[:], offs2)
+        load_scale_rows(key_scale_table, tab_scales)
         nc.sync.dma_start(key_list[:], offs)
         load_scale_rows(query_scale_table, tab2_scales)
-        load_scale_rows(key_scale_table, tab_scales)
-        load_words(key_table[0], tab_words[0], slice(KEY_HEAD, T))
-        load_words(key_table[1], tab_words[1], slice(0, T))
+        nc.sync.dma_start(query_list[:], offs2)
+        for a in range(PASSES):
+            load_words(key_table[a], tab_words[a], slice(0, T))
 
         key_scales = tile("key_scales", [P, S], U8)
         query_scales = tile("query_scales", [P, S2], U8)
         scale_rows = tile("scale_rows", [P, (S + S2) // BYTES_PER_I32], I32)
-        nc.vector.tensor_copy(query_scales[:], query_scale_table[:].bitcast(U8).indirect(query_list[:]))
         nc.vector.tensor_copy(key_scales[:], key_scale_table[:].bitcast(U8).indirect(key_list[:]))
-        nc.vector.tensor_copy(scale_rows[:, S // BYTES_PER_I32:], query_scales[:].bitcast(I32))
+        nc.vector.tensor_copy(query_scales[:], query_scale_table[:].bitcast(U8).indirect(query_list[:]))
         nc.vector.tensor_copy(scale_rows[:].bitcast(U8)[:, :S].rearrange("p (b t m) -> p b t m", b=PASSES, t=PACK),
                               key_scales[:].rearrange("p (b m t) -> p b t m", b=PASSES, t=PACK))
+        nc.vector.tensor_copy(scale_rows[:, S // BYTES_PER_I32:], query_scales[:].bitcast(I32))
 
-        def move_to_planes(a, queue):
-            first = SPREAD * BLOCKS * a
+        def move_to_planes(a):
+            first = BLOCKS * a
             for r in range(QUAD_ROWS):
-                queue.dma_start(
+                nc.sync.dma_start(
                     out=planes[a][QUAD_ROWS * a + r:P:QUAD, :],
-                    in_=scale_rows[first + SPREAD * r: first + SPREAD * BLOCKS: SPREAD * QUAD_ROWS, :])
+                    in_=scale_rows[first + r: first + BLOCKS: QUAD_ROWS, :])
 
-        for a, queue in enumerate((nc.sync, nc.gpsimd)):
-            move_to_planes(a, queue)
+        for a in range(PASSES):
+            move_to_planes(a)
             load_words(query_table[a], tab2_words[a], slice(0, T2))
 
         keys = [tile("keys%d" % a, [P, S], U32) for a in range(PASSES)]

@@ -28,14 +28,22 @@ LIST_GROUP = 16
 BYTES_PER_I32 = 4
 HALVES = 2
 HALF = S2 // HALVES
-QUARTER = HALF // 2
+QUARTERS = 2 * HALVES
+QUARTER = S2 // QUARTERS
 RUN = 2
 BANKS = 8
 SCORE_BANKS = 3
 CHUNK = 2 * P
 CHUNKS = N // CHUNK
 
-REUSES = {"wg_bf1": "att0_1", "wg_bf2": "att1_0"}
+REUSES = {
+    "wg_bf1_0": "queries1",
+    "wg_bf1_1": "keys1",
+    "wg_bf2_0": "att2",
+    "wg_bf2_1": "att3",
+    "wg_plane0_1": "h_bf1",
+    "h_bf3": "wg_bf0_1",
+}
 
 
 def tile_list_beam_sigmoid_glu_kernel(tc, tab_words, tab_scales, tab2_words, tab2_scales,
@@ -132,18 +140,16 @@ def tile_list_beam_sigmoid_glu_kernel(tc, tab_words, tab_scales, tab2_words, tab
         for c in range(1, CHUNKS):
             load_wg(c)
 
-        att = {}
-        for h in range(HALVES):
-            for b in range(PASSES):
-                att[h, b] = tile("att%d_%d" % (h, b), [P, HALF, PACK], F32)
-        h_bf = [tile("h_bf%d" % h, [P, PASSES * HALF * PACK], BF16) for h in range(HALVES)]
+        att = [tile("att%d" % q, [P, PASSES, QUARTER, PACK], F32) for q in range(QUARTERS)]
+        h_bf = [tile("h_bf%d" % q, [P, PASSES, QUARTER * PACK], BF16) for q in range(QUARTERS)]
         h_codes = [tile("h_codes%d" % h, [P, PASSES * HALF], U32) for h in range(HALVES)]
         h_plane = [tile("h_plane%d" % h, [P, PASSES * HALF], U8) for h in range(HALVES)]
-        wg_bf = [tile("wg_bf%d" % c, [P, PASSES * CHUNK * PACK], BF16) for c in range(CHUNKS)]
-        wg_codes = [tile("wg_codes%d" % c, [P, PASSES * CHUNK], U32) for c in range(CHUNKS)]
-        wg_plane = [tile("wg_plane%d" % c, [P, PASSES * CHUNK], U8) for c in range(CHUNKS)]
+        pieces = [(c, b) for c in range(CHUNKS) for b in range(PASSES)]
+        wg_bf = {(c, b): tile("wg_bf%d_%d" % (c, b), [P, CHUNK * PACK], BF16) for c, b in pieces}
+        wg_codes = {(c, b): tile("wg_codes%d_%d" % (c, b), [P, CHUNK], U32) for c, b in pieces}
+        wg_plane = {(c, b): tile("wg_plane%d_%d" % (c, b), [P, CHUNK], U8) for c, b in pieces}
 
-        def score_pass(acc, b, quarter, a):
+        def score_pass(acc, b, q, a):
             plane = planes[a][QUAD_ROWS * a:, :].bitcast(U8)
             for t in range(PACK):
                 u = PACK * b + t
@@ -151,58 +157,52 @@ def tile_list_beam_sigmoid_glu_kernel(tc, tab_words, tab_scales, tab2_words, tab
                     out=acc[:, QUARTER * t: QUARTER * (t + 1)],
                     lhsT=keys[a][:, P * u: P * (u + 1)].bitcast(FP8X4),
                     lhsT_scale=plane[:, P * u: P * (u + 1)],
-                    rhs=queries[a][:, QUARTER * quarter: QUARTER * (quarter + 1)].bitcast(FP8X4),
-                    rhs_scale=plane[:, S + QUARTER * quarter: S + QUARTER * (quarter + 1)],
+                    rhs=queries[a][:, QUARTER * q: QUARTER * (q + 1)].bitcast(FP8X4),
+                    rhs_scale=plane[:, S + QUARTER * q: S + QUARTER * (q + 1)],
                     start=(a == 0 and t == 0), stop=(a == PASSES - 1 and t == PACK - 1))
 
-        def weigh(h, b):
-            factor = conf_sb[:, b, :].unsqueeze(1).to_broadcast([P, HALF, PACK])
-            dst = h_bf[h][:, HALF * PACK * b: HALF * PACK * (b + 1)].rearrange("p (j t) -> p j t", t=PACK)
-            nc.vector.tensor_tensor(dst, att[h, b][:], factor, MULT)
+        def h_cols(q, b):
+            first = HALF * b + QUARTER * (q % 2)
+            return slice(first, first + QUARTER)
 
-        def quantise(codes, plane, rounded, first, last):
-            width = codes.shape[1] // PASSES
-            cols = slice(width * first, width * last)
-            nc.vector.quantize_mx(out=codes[:, cols].bitcast(FP8X4), scales=plane[:, cols],
-                                  in_=rounded[:, width * PACK * first: width * PACK * last])
+        def weigh(q):
+            factor = conf_sb[:].unsqueeze(2).to_broadcast([P, PASSES, QUARTER, PACK])
+            nc.vector.tensor_tensor(h_bf[q][:].rearrange("p b (j t) -> p b j t", t=PACK), att[q][:], factor, MULT)
 
-        def make_h(h):
+        def quantise_h(q):
             for b in range(PASSES):
-                weigh(h, b)
-            for b in range(PASSES):
-                quantise(h_codes[h], h_plane[h], h_bf[h], b, b + 1)
+                nc.vector.quantize_mx(out=h_codes[q // 2][:, h_cols(q, b)].bitcast(FP8X4),
+                                      scales=h_plane[q // 2][:, h_cols(q, b)], in_=h_bf[q][:, b, :])
 
-        def quantise_wg(c, first=0, last=PASSES):
-            quantise(wg_codes[c], wg_plane[c], wg_bf[c], first, last)
+        def quantise_wg(c, b):
+            nc.vector.quantize_mx(out=wg_codes[c, b][:].bitcast(FP8X4), scales=wg_plane[c, b][:], in_=wg_bf[c, b][:])
 
         def round_wg(c, b, copy):
-            dst = wg_bf[c][:, CHUNK * PACK * b: CHUNK * PACK * (b + 1)]
-            copy(dst.rearrange("p (x y t) -> p x t y", y=RUN, t=PACK),
+            copy(wg_bf[c, b][:].rearrange("p (x y t) -> p x t y", y=RUN, t=PACK),
                  wg_f32[c, b][:].rearrange("p t (x y) -> p x t y", y=RUN))
 
         def gate(h, c, acc):
             for m in range(CHUNK // P):
                 for b in range(PASSES):
-                    cols = slice(CHUNK * b + P * m, CHUNK * b + P * (m + 1))
+                    cols = slice(P * m, P * (m + 1))
                     picked = slice(HALF * b, HALF * (b + 1))
                     nc.tensor.matmul_mx(
                         out=acc[:, HALF * m: HALF * (m + 1)],
-                        lhsT=wg_codes[c][:, cols].bitcast(FP8X4), lhsT_scale=wg_plane[c][:, cols],
+                        lhsT=wg_codes[c, b][:, cols].bitcast(FP8X4), lhsT_scale=wg_plane[c, b][:, cols],
                         rhs=h_codes[h][:, picked].bitcast(FP8X4), rhs_scale=h_plane[h][:, picked],
                         start=(b == 0), stop=(b == PASSES - 1))
 
-        def context(h, c, acc):
+        def context(q, c, acc):
             for m in range(CHUNK // P):
                 n0 = CHUNK * c + P * m
-                for j in range(0, HALF, P):
-                    for b in range(PASSES):
-                        picked = slice(HALF * b + j, HALF * b + j + P)
-                        nc.tensor.matmul_mx(
-                            out=acc[:, HALF * m + j: HALF * m + j + P],
-                            lhsT=w4_codes[:, b, n0 // 2: (n0 + P) // 2].bitcast(U8).bitcast(FP4X4),
-                            lhsT_scale=w4_planes[:, b, n0 // BYTES_PER_I32: (n0 + P) // BYTES_PER_I32].bitcast(U8),
-                            rhs=h_codes[h][:, picked].bitcast(FP8X4), rhs_scale=h_plane[h][:, picked],
-                            start=(b == 0), stop=(b == PASSES - 1))
+                first = HALF * m + QUARTER * (q % 2)
+                for b in range(PASSES):
+                    nc.tensor.matmul_mx(
+                        out=acc[:, first: first + QUARTER],
+                        lhsT=w4_codes[:, b, n0 // 2: (n0 + P) // 2].bitcast(U8).bitcast(FP4X4),
+                        lhsT_scale=w4_planes[:, b, n0 // BYTES_PER_I32: (n0 + P) // BYTES_PER_I32].bitcast(U8),
+                        rhs=h_codes[q // 2][:, h_cols(q, b)].bitcast(FP8X4), rhs_scale=h_plane[q // 2][:, h_cols(q, b)],
+                        start=(b == 0), stop=(b == PASSES - 1))
 
         def finish(name, gate_sum, context_sum, dst):
             gate_sig = tile("gate_sig" + name, [P, gate_sum.shape[1]], F32)
@@ -214,52 +214,73 @@ def tile_list_beam_sigmoid_glu_kernel(tc, tab_words, tab_scales, tab2_words, tab
         def out_rows(h, c):
             return out[CHUNK * c: CHUNK * (c + 1), HALF * h: HALF * (h + 1)].rearrange("(m p) j -> p m j", p=P)
 
-        scores = [(h, b, x) for h in range(HALVES) for b in range(PASSES) for x in range(HALF // QUARTER)]
-        for number, (h, b, x) in enumerate(scores):
+        scores = [(q, b) for q in range(QUARTERS) for b in range(PASSES)]
+        for number, (q, b) in enumerate(scores):
             acc = bank(number % SCORE_BANKS)
             for a in range(PASSES):
-                score_pass(acc, b, HALF // QUARTER * h + x, a)
-            nc.scalar.activation(att[h, b][:, QUARTER * x: QUARTER * (x + 1), :],
-                                 acc[:].rearrange("p (t j) -> p j t", t=PACK), SIGMOID)
+                score_pass(acc, b, q, a)
+            nc.scalar.activation(att[q][:, b, :, :], acc[:].rearrange("p (t j) -> p j t", t=PACK), SIGMOID)
 
         free = list(range(SCORE_BANKS, BANKS))
         free.extend(number % SCORE_BANKS for number in range(len(scores) - SCORE_BANKS, len(scores)))
-        waiting = [(h, c) for c in range(CHUNKS) for h in range(HALVES)]
         sums = {}
 
-        def finish_oldest():
-            h, c = waiting.pop(0)
+        def sum_bank(step, h, c):
+            if (step, h, c) not in sums:
+                number = free.pop(0)
+                sums[step, h, c] = (number, bank(number))
+            return sums[step, h, c][1]
+
+        def do_gate(h, c):
+            gate(h, c, sum_bank(gate, h, c))
+
+        def do_context(q, c):
+            context(q, c, sum_bank(context, q // 2, c))
+
+        def finish_unit(h, c):
             finish("%d_%d" % (h, c), sums[gate, h, c][1][:], sums[context, h, c][1][:], out_rows(h, c))
             free.extend((sums[gate, h, c][0], sums[context, h, c][0]))
 
-        def multiply(step, h, c):
-            if not free:
-                finish_oldest()
-            number = free.pop(0)
-            sums[step, h, c] = (number, bank(number))
-            step(h, c, sums[step, h, c][1])
-
         on_vector, on_scalar = nc.vector.tensor_copy, nc.scalar.copy
         round_wg(0, 0, on_vector)
-        quantise_wg(0, 0, 1)
+        quantise_wg(0, 0)
         round_wg(0, 1, on_vector)
-        make_h(0)
+        weigh(0)
+        weigh(1)
+        for q in range(2):
+            quantise_h(q)
+            for c in range(CHUNKS):
+                do_context(q, c)
+        round_wg(1, 0, on_scalar)
+        round_wg(1, 1, on_scalar)
+        weigh(2)
+        quantise_wg(0, 1)
+        do_gate(0, 0)
+        quantise_h(2)
         for c in range(CHUNKS):
-            multiply(context, 0, c)
-        make_h(1)
-        quantise_wg(0, 1, PASSES)
-
-        for c in range(CHUNKS):
-            if c > 0:
-                round_wg(c, 0, on_scalar)
-                round_wg(c, 1, on_vector if c == CHUNKS - 1 else on_scalar)
-                quantise_wg(c)
-            for h in range(HALVES):
-                multiply(gate, h, c)
-            multiply(context, 1, c)
-        for unit in range(len(waiting) - 1):
-            finish_oldest()
-        h, c = waiting.pop(0)
+            do_context(2, c)
+        weigh(3)
+        quantise_wg(1, 0)
+        quantise_h(3)
+        do_gate(1, 0)
+        do_context(3, 0)
+        quantise_wg(1, 1)
+        finish_unit(0, 0)
+        round_wg(2, 0, on_scalar)
+        round_wg(2, 1, on_vector)
+        do_gate(0, 1)
+        do_gate(1, 1)
+        do_context(3, 1)
+        quantise_wg(2, 0)
+        quantise_wg(2, 1)
+        finish_unit(1, 0)
+        do_gate(0, 2)
+        do_gate(1, 2)
+        do_context(3, 2)
+        finish_unit(0, 1)
+        finish_unit(1, 1)
+        finish_unit(0, 2)
+        h, c = HALVES - 1, CHUNKS - 1
         for m in range(CHUNK // P):
             cols = slice(HALF * m, HALF * (m + 1))
             finish("%d_%d_%d" % (h, c, m), sums[gate, h, c][1][:, cols], sums[context, h, c][1][:, cols],

@@ -1,6 +1,7 @@
 from contextlib import ExitStack
 
 import concourse.mybir as mybir
+from concourse.masks import make_identity
 
 K, T, S, T2, S2, N = 1024, 4096, 1024, 2048, 512, 768
 FLOPS = 2 * K * S * S2 + 2 * 2 * S * N * S2
@@ -15,6 +16,7 @@ FP8X4 = mybir.dt.float8_e4m3fn_x4
 FP4X4 = mybir.dt.float4_e2m1fn_x4
 SIGMOID = mybir.ActivationFunctionType.Sigmoid
 MULT = mybir.AluOpType.mult
+ADD = mybir.AluOpType.add
 
 P = 128
 PACK = 4
@@ -37,13 +39,17 @@ CHUNK = 2 * P
 CHUNKS = N // CHUNK
 
 REUSES = {
-    "wg_bf1_0": "queries1",
-    "wg_bf1_1": "keys1",
-    "wg_bf2_0": "att2",
-    "wg_bf2_1": "att3",
-    "wg_plane0_1": "h_bf1",
-    "h_bf3": "wg_bf0_1",
+    "wg_bf0_1": "wg_bf0_0",
+    "wg_plane0_1": "h_bf0",
+    "wg_bf1_0_0": "h_bf1",
+    "wg_bf1_0_1": "h_bf2",
+    "wg_bf1_1": "queries1",
+    "wg_bf2_0": "keys1",
+    "wg_bf2_1_0": "att2",
+    "wg_bf2_1_1": "wg_bf1_0_1",
+    "h_bf3": "wg_bf0_0",
 }
+SPLIT = ((1, 0), (2, 1))
 
 
 def tile_list_beam_sigmoid_glu_kernel(tc, tab_words, tab_scales, tab2_words, tab2_scales,
@@ -53,8 +59,11 @@ def tile_list_beam_sigmoid_glu_kernel(tc, tab_words, tab_scales, tab2_words, tab
         keep = ctx.enter_context(tc.tile_pool(name="keep", bufs=1))
         psum = ctx.enter_context(tc.psum_pool(name="psum", bufs=1))
 
+        def owner(name):
+            return owner(REUSES[name]) if name in REUSES else name
+
         def tile(name, shape, dtype):
-            return keep.tile(shape, dtype, name=name, tag=REUSES.get(name, name), align_bytes=64)
+            return keep.tile(shape, dtype, name=name, tag=owner(name), align_bytes=64)
 
         def bank(number):
             return psum.tile([P, 2 * HALF], F32, name="bank%d" % number)
@@ -87,6 +96,10 @@ def tile_list_beam_sigmoid_glu_kernel(tc, tab_words, tab_scales, tab2_words, tab
         nc.sync.dma_start(key_list[:], offs)
         load_scale_rows(query_scale_table, tab2_scales)
         nc.sync.dma_start(query_list[:], offs2)
+        conf_sb = tile("conf_sb", [P, P], F32)
+        nc.vector.memset(conf_sb[:, PASSES * PACK:], 0.0)
+        nc.sync.dma_start(out=conf_sb[:, :PASSES * PACK].rearrange("p (b t) -> p b t", t=PACK),
+                          in_=conf.rearrange("(b p t) -> p b t", b=PASSES, t=PACK))
         for a in range(PASSES):
             load_words(key_table[a], tab_words[a], slice(0, T))
 
@@ -122,30 +135,42 @@ def tile_list_beam_sigmoid_glu_kernel(tc, tab_words, tab_scales, tab2_words, tab
                     queries[a][:, HALF * h: HALF * (h + 1)],
                     query_table[a][:].bitcast(U32).indirect(query_list[:, list_cols * h: list_cols * (h + 1)]))
 
+        identity = tile("identity", [P, P], F32)
+        make_identity(nc, identity[:])
+        turned = bank(BANKS - 2)
+        nc.tensor.transpose(turned[:, :P], conf_sb[:], identity[:])
+        conf_rows = tile("conf_rows", [P, P], F32)
+        nc.vector.tensor_copy(conf_rows[:], turned[:, :P])
+        conf_bank = bank(BANKS - 1)
+        nc.tensor.transpose(conf_bank[:, :P], conf_rows[:], identity[:])
+
         wg_f32 = {}
 
-        def load_wg(c):
-            for b in range(PASSES):
-                wg_f32[c, b] = tile("wg_f32_%d_%d" % (c, b), [P, PACK, CHUNK], F32)
-                rows = wg[PASS_LEN * b: PASS_LEN * (b + 1), CHUNK * c: CHUNK * (c + 1)]
-                nc.sync.dma_start(out=wg_f32[c, b][:], in_=rows.rearrange("(p t) n -> p t n", t=PACK))
+        def load_wg(c, b):
+            wg_f32[c, b] = tile("wg_f32_%d_%d" % (c, b), [P, PACK, CHUNK], F32)
+            rows = wg[PASS_LEN * b: PASS_LEN * (b + 1), CHUNK * c: CHUNK * (c + 1)]
+            nc.sync.dma_start(out=wg_f32[c, b][:], in_=rows.rearrange("(p t) n -> p t n", t=PACK))
 
-        conf_sb = tile("conf_sb", [P, PASSES, PACK], F32)
-        nc.sync.dma_start(out=conf_sb[:], in_=conf.rearrange("(b p t) -> p b t", b=PASSES, t=PACK))
-        load_wg(0)
+        load_wg(0, 0)
+        load_wg(0, 1)
         nc.sync.dma_start(out=w4_codes, in_=w4_words.rearrange("b p e -> p b e").bitcast(I32))
         for r in range(QUAD_ROWS):
             nc.sync.dma_start(out=w4_planes[r:P:QUAD, :, :],
                               in_=w4_scales[:, r:BLOCKS:QUAD_ROWS, :].rearrange("b q n -> q b n").bitcast(I32))
-        for c in range(1, CHUNKS):
-            load_wg(c)
+        load_wg(1, 0)
+        load_wg(1, 1)
+        load_wg(2, 0)
+        load_wg(2, 1)
 
         att = [tile("att%d" % q, [P, PASSES, QUARTER, PACK], F32) for q in range(QUARTERS)]
         h_bf = [tile("h_bf%d" % q, [P, PASSES, QUARTER * PACK], BF16) for q in range(QUARTERS)]
         h_codes = [tile("h_codes%d" % h, [P, PASSES * HALF], U32) for h in range(HALVES)]
         h_plane = [tile("h_plane%d" % h, [P, PASSES * HALF], U8) for h in range(HALVES)]
         pieces = [(c, b) for c in range(CHUNKS) for b in range(PASSES)]
-        wg_bf = {(c, b): tile("wg_bf%d_%d" % (c, b), [P, CHUNK * PACK], BF16) for c, b in pieces}
+        wg_bf = {(c, b): tile("wg_bf%d_%d" % (c, b), [P, CHUNK * PACK], BF16)
+                 for c, b in pieces if (c, b) not in SPLIT}
+        wg_bf.update({(c, b, m): tile("wg_bf%d_%d_%d" % (c, b, m), [P, P * PACK], BF16)
+                      for c, b in SPLIT for m in range(CHUNK // P)})
         wg_codes = {(c, b): tile("wg_codes%d_%d" % (c, b), [P, CHUNK], U32) for c, b in pieces}
         wg_plane = {(c, b): tile("wg_plane%d_%d" % (c, b), [P, CHUNK], U8) for c, b in pieces}
 
@@ -166,7 +191,7 @@ def tile_list_beam_sigmoid_glu_kernel(tc, tab_words, tab_scales, tab2_words, tab
             return slice(first, first + QUARTER)
 
         def weigh(q):
-            factor = conf_sb[:].unsqueeze(2).to_broadcast([P, PASSES, QUARTER, PACK])
+            factor = conf_bank[:, :PASSES * PACK].rearrange("p (b t) -> p b t", t=PACK).unsqueeze(2).to_broadcast([P, PASSES, QUARTER, PACK])
             nc.vector.tensor_tensor(h_bf[q][:].rearrange("p b (j t) -> p b j t", t=PACK), att[q][:], factor, MULT)
 
         def quantise_h(q):
@@ -174,12 +199,21 @@ def tile_list_beam_sigmoid_glu_kernel(tc, tab_words, tab_scales, tab2_words, tab
                 nc.vector.quantize_mx(out=h_codes[q // 2][:, h_cols(q, b)].bitcast(FP8X4),
                                       scales=h_plane[q // 2][:, h_cols(q, b)], in_=h_bf[q][:, b, :])
 
-        def quantise_wg(c, b):
-            nc.vector.quantize_mx(out=wg_codes[c, b][:].bitcast(FP8X4), scales=wg_plane[c, b][:], in_=wg_bf[c, b][:])
+        def channels(piece):
+            return slice(0, CHUNK) if len(piece) == 2 else slice(P * piece[2], P * (piece[2] + 1))
 
-        def round_wg(c, b, copy):
-            copy(wg_bf[c, b][:].rearrange("p (x y t) -> p x t y", y=RUN, t=PACK),
-                 wg_f32[c, b][:].rearrange("p t (x y) -> p x t y", y=RUN))
+        def quantise_wg(*piece):
+            nc.vector.quantize_mx(out=wg_codes[piece[:2]][:, channels(piece)].bitcast(FP8X4),
+                                  scales=wg_plane[piece[:2]][:, channels(piece)], in_=wg_bf[piece][:])
+
+        def round_wg(copy, *piece):
+            copy(wg_bf[piece][:].rearrange("p (x y t) -> p x t y", y=RUN, t=PACK),
+                 wg_f32[piece[:2]][:, :, channels(piece)].rearrange("p t (x y) -> p x t y", y=RUN))
+
+        def round_on_gpsimd(*piece):
+            nc.gpsimd.tensor_scalar(wg_bf[piece][:].rearrange("p (x t) -> p x t", t=PACK),
+                                    wg_f32[piece[:2]][:, :, channels(piece)].rearrange("p t x -> p x t"),
+                                    1.0, 0.0, MULT, ADD)
 
         def gate(h, c, acc):
             for m in range(CHUNK // P):
@@ -221,8 +255,9 @@ def tile_list_beam_sigmoid_glu_kernel(tc, tab_words, tab_scales, tab2_words, tab
                 score_pass(acc, b, q, a)
             nc.scalar.activation(att[q][:, b, :, :], acc[:].rearrange("p (t j) -> p j t", t=PACK), SIGMOID)
 
-        free = list(range(SCORE_BANKS, BANKS))
+        free = list(range(SCORE_BANKS, BANKS - 1))
         free.extend(number % SCORE_BANKS for number in range(len(scores) - SCORE_BANKS, len(scores)))
+        free.append(BANKS - 1)
         sums = {}
 
         def sum_bank(step, h, c):
@@ -242,37 +277,41 @@ def tile_list_beam_sigmoid_glu_kernel(tc, tab_words, tab_scales, tab2_words, tab
             free.extend((sums[gate, h, c][0], sums[context, h, c][0]))
 
         on_vector, on_scalar = nc.vector.tensor_copy, nc.scalar.copy
-        round_wg(0, 0, on_vector)
+        round_wg(on_vector, 0, 0)
         quantise_wg(0, 0)
-        round_wg(0, 1, on_vector)
+        round_on_gpsimd(0, 1)
         weigh(0)
         weigh(1)
         for q in range(2):
             quantise_h(q)
             for c in range(CHUNKS):
                 do_context(q, c)
-        round_wg(1, 0, on_scalar)
-        round_wg(1, 1, on_scalar)
+        round_on_gpsimd(1, 0, 0)
+        round_wg(on_scalar, 1, 1)
+        round_wg(on_scalar, 2, 0)
         weigh(2)
         quantise_wg(0, 1)
         do_gate(0, 0)
         quantise_h(2)
+        round_on_gpsimd(1, 0, 1)
         for c in range(CHUNKS):
             do_context(2, c)
         weigh(3)
-        quantise_wg(1, 0)
+        quantise_wg(1, 0, 0)
         quantise_h(3)
         do_gate(1, 0)
         do_context(3, 0)
+        quantise_wg(1, 0, 1)
         quantise_wg(1, 1)
         finish_unit(0, 0)
-        round_wg(2, 0, on_scalar)
-        round_wg(2, 1, on_vector)
+        round_wg(on_vector, 2, 1, 1)
+        round_wg(on_scalar, 2, 1, 0)
         do_gate(0, 1)
         do_gate(1, 1)
         do_context(3, 1)
         quantise_wg(2, 0)
-        quantise_wg(2, 1)
+        quantise_wg(2, 1, 1)
+        quantise_wg(2, 1, 0)
         finish_unit(1, 0)
         do_gate(0, 2)
         do_gate(1, 2)

@@ -34,7 +34,7 @@ QUARTERS = 2 * HALVES
 QUARTER = S2 // QUARTERS
 RUN = 2
 BANKS = 8
-SCORE_BANKS = 3
+SCORE_BANKS = 4
 CHUNK = 2 * P
 CHUNKS = N // CHUNK
 
@@ -63,7 +63,7 @@ def tile_list_beam_sigmoid_glu_kernel(tc, tab_words, tab_scales, tab2_words, tab
             return owner(REUSES[name]) if name in REUSES else name
 
         def tile(name, shape, dtype):
-            return keep.tile(shape, dtype, name=name, tag=owner(name), align_bytes=64)
+            return keep.tile(shape, dtype, name=name, tag=owner(name), align_bytes=256)
 
         def bank(number):
             return psum.tile([P, 2 * HALF], F32, name="bank%d" % number)
@@ -112,15 +112,15 @@ def tile_list_beam_sigmoid_glu_kernel(tc, tab_words, tab_scales, tab2_words, tab
                               key_scales[:].rearrange("p (b m t) -> p b t m", b=PASSES, t=PACK))
         nc.vector.tensor_copy(scale_rows[:, S // BYTES_PER_I32:], query_scales[:].bitcast(I32))
 
-        def move_to_planes(a):
+        def move_to_planes(a, queue):
             first = BLOCKS * a
             for r in range(QUAD_ROWS):
-                nc.sync.dma_start(
+                queue.dma_start(
                     out=planes[a][QUAD_ROWS * a + r:P:QUAD, :],
                     in_=scale_rows[first + r: first + BLOCKS: QUAD_ROWS, :])
 
-        for a in range(PASSES):
-            move_to_planes(a)
+        for a, queue in enumerate((nc.sync, nc.gpsimd)):
+            move_to_planes(a, queue)
             load_words(query_table[a], tab2_words[a], slice(0, T2))
 
         keys = [tile("keys%d" % a, [P, S], U32) for a in range(PASSES)]
@@ -318,9 +318,9 @@ def tile_list_beam_sigmoid_glu_kernel(tc, tab_words, tab_scales, tab2_words, tab
         do_context(3, 2)
         finish_unit(0, 1)
         finish_unit(1, 1)
-        finish_unit(0, 2)
-        h, c = HALVES - 1, CHUNKS - 1
-        for m in range(CHUNK // P):
-            cols = slice(HALF * m, HALF * (m + 1))
-            finish("%d_%d_%d" % (h, c, m), sums[gate, h, c][1][:, cols], sums[context, h, c][1][:, cols],
-                   out_rows(h, c)[:, m: m + 1, :])
+        c = CHUNKS - 1
+        for h in range(HALVES):
+            for m in range(CHUNK // P):
+                cols = slice(HALF * m, HALF * (m + 1))
+                finish("%d_%d_%d" % (h, c, m), sums[gate, h, c][1][:, cols], sums[context, h, c][1][:, cols],
+                       out_rows(h, c)[:, m: m + 1, :])

@@ -28,32 +28,28 @@ QUAD_ROWS = 4
 SCALE_ROWS = PASSES * BLOCKS
 LIST_GROUP = 16
 BYTES_PER_I32 = 4
-HALVES = 2
-HALF = S2 // HALVES
-QUARTERS = 2 * HALVES
+HALF = S2 // 2
+QUARTERS = 4
 QUARTER = S2 // QUARTERS
 RUN = 2
-BANKS = 8
 SCORE_BANKS = 4
+CONF_BANK = 7
+TILES = N // P
 CHUNK = 2 * P
 CHUNKS = N // CHUNK
 
 REUSES = {
-    "wg_bf0_1": "wg_bf0_0",
-    "wg_plane0_1": "h_bf0",
-    "wg_bf1_0_0": "h_bf1",
-    "wg_bf1_0_1": "h_bf2",
-    "wg_bf1_1": "queries1",
-    "wg_bf2_0": "keys1",
-    "wg_bf2_1_0": "att2",
-    "wg_bf2_1_1": "wg_bf1_0_1",
-    "h_bf3": "wg_bf0_0",
+    "h_codes0": "wg_f32_0_0",
+    "wg_bf0_1": "h_bf0_0",
+    "wg_plane0_0": "wg_f32_0_1",
+    "h_bf1_1": "h_bf0_1",
+    "wg_bf3_1": "h_bf1_0",
+    "wg_bf4_1": "wg_bf4_0",
 }
-SPLIT = ((1, 0), (2, 1))
 
 
 def tile_list_beam_sigmoid_glu_kernel(tc, tab_words, tab_scales, tab2_words, tab2_scales,
-                                               w4_words, w4_scales, wg, conf, offs, offs2, out):
+                                                   w4_words, w4_scales, wg, conf, offs, offs2, out):
     nc = tc.nc
     with ExitStack() as ctx:
         keep = ctx.enter_context(tc.tile_pool(name="keep", bufs=1))
@@ -66,7 +62,7 @@ def tile_list_beam_sigmoid_glu_kernel(tc, tab_words, tab_scales, tab2_words, tab
             return keep.tile(shape, dtype, name=name, tag=owner(name), align_bytes=256)
 
         def bank(number):
-            return psum.tile([P, 2 * HALF], F32, name="bank%d" % number)
+            return psum.tile([P, S2], F32, name="bank%d" % number)
 
         key_list = keep.tile([P, S // LIST_GROUP], U16, name="key_list")
         query_list = keep.tile([P, S2 // LIST_GROUP], U16, name="query_list")
@@ -75,19 +71,20 @@ def tile_list_beam_sigmoid_glu_kernel(tc, tab_words, tab_scales, tab2_words, tab
         key_scale_table = tile("key_scale_table", [P, T // BYTES_PER_I32], I32)
         query_scale_table = tile("query_scale_table", [P, T2 // BYTES_PER_I32], I32)
         planes = [tile("planes%d" % a, [P, (S + S2) // BYTES_PER_I32], I32) for a in range(PASSES)]
-        w4 = tile("w4", [P, PASSES * (N // 2 + N // BYTES_PER_I32)], I32)
-        w4_codes = w4[:, :N].rearrange("p (b e) -> p b e", b=PASSES)
-        w4_planes = w4[:, N:].rearrange("p (b e) -> p b e", b=PASSES)
+        w4_codes = tile("w4_codes", [P, PASSES, N // 2], I32)
+        w4_planes = tile("w4_planes", [P, PASSES, N // BYTES_PER_I32], I32)
+        conf_row = tile("conf_row", [P, S], F32)
 
         for rows in (slice(QUAD, 2 * QUAD), slice(2 * QUAD, P)):
             nc.vector.memset(key_scale_table[rows, :], 0)
             nc.gpsimd.memset(query_scale_table[rows, :], 0)
+        nc.gpsimd.memset(conf_row[:], 0.0)
+        nc.gpsimd.memset(w4_planes[:], 0)
         for a in range(PASSES):
             nc.vector.memset(planes[a][:], 0)
-        nc.gpsimd.memset(w4_planes, 0)
 
-        def load_words(dst, words, cols):
-            nc.sync.dma_start(out=dst[:, cols], in_=words.rearrange("p t i -> p (t i)").bitcast(I32)[:, cols])
+        def load_words(dst, words):
+            nc.sync.dma_start(out=dst[:], in_=words.rearrange("p t i -> p (t i)").bitcast(I32))
 
         def load_scale_rows(dst, scales):
             nc.sync.dma_start(out=dst[:SCALE_ROWS, :], in_=scales.rearrange("a q t -> (a q) t").bitcast(I32))
@@ -96,12 +93,12 @@ def tile_list_beam_sigmoid_glu_kernel(tc, tab_words, tab_scales, tab2_words, tab
         nc.sync.dma_start(key_list[:], offs)
         load_scale_rows(query_scale_table, tab2_scales)
         nc.sync.dma_start(query_list[:], offs2)
-        conf_sb = tile("conf_sb", [P, P], F32)
-        nc.vector.memset(conf_sb[:, PASSES * PACK:], 0.0)
-        nc.sync.dma_start(out=conf_sb[:, :PASSES * PACK].rearrange("p (b t) -> p b t", t=PACK),
-                          in_=conf.rearrange("(b p t) -> p b t", b=PASSES, t=PACK))
-        for a in range(PASSES):
-            load_words(key_table[a], tab_words[a], slice(0, T))
+        load_words(key_table[0], tab_words[0])
+        nc.sync.dma_start(out=conf_row[:1, :], in_=conf.rearrange("(o i) -> o i", o=1))
+        load_words(key_table[1], tab_words[1])
+        for r in range(QUAD_ROWS):
+            nc.gpsimd.dma_start(out=w4_planes[r:P:QUAD, :, :],
+                                in_=w4_scales[:, r:BLOCKS:QUAD_ROWS, :].rearrange("b q n -> q b n").bitcast(I32))
 
         key_scales = tile("key_scales", [P, S], U8)
         query_scales = tile("query_scales", [P, S2], U8)
@@ -112,37 +109,12 @@ def tile_list_beam_sigmoid_glu_kernel(tc, tab_words, tab_scales, tab2_words, tab
                               key_scales[:].rearrange("p (b m t) -> p b t m", b=PASSES, t=PACK))
         nc.vector.tensor_copy(scale_rows[:, S // BYTES_PER_I32:], query_scales[:].bitcast(I32))
 
-        def move_to_planes(a, queue):
+        for a in range(PASSES):
             first = BLOCKS * a
             for r in range(QUAD_ROWS):
-                queue.dma_start(
-                    out=planes[a][QUAD_ROWS * a + r:P:QUAD, :],
-                    in_=scale_rows[first + r: first + BLOCKS: QUAD_ROWS, :])
-
-        for a, queue in enumerate((nc.sync, nc.gpsimd)):
-            move_to_planes(a, queue)
-            load_words(query_table[a], tab2_words[a], slice(0, T2))
-
-        keys = [tile("keys%d" % a, [P, S], U32) for a in range(PASSES)]
-        queries = [tile("queries%d" % a, [P, S2], U32) for a in range(PASSES)]
-        for a in range(PASSES):
-            nc.vector.tensor_copy(keys[a][:].rearrange("p (b t m) -> p b m t", b=PASSES, t=PACK),
-                                  key_table[a][:].bitcast(U32).indirect(key_list[:]))
-        list_cols = HALF // LIST_GROUP
-        for a in range(PASSES):
-            for h in range(HALVES):
-                nc.vector.tensor_copy(
-                    queries[a][:, HALF * h: HALF * (h + 1)],
-                    query_table[a][:].bitcast(U32).indirect(query_list[:, list_cols * h: list_cols * (h + 1)]))
-
-        identity = tile("identity", [P, P], F32)
-        make_identity(nc, identity[:])
-        turned = bank(BANKS - 2)
-        nc.tensor.transpose(turned[:, :P], conf_sb[:], identity[:])
-        conf_rows = tile("conf_rows", [P, P], F32)
-        nc.vector.tensor_copy(conf_rows[:], turned[:, :P])
-        conf_bank = bank(BANKS - 1)
-        nc.tensor.transpose(conf_bank[:, :P], conf_rows[:], identity[:])
+                nc.sync.dma_start(out=planes[a][QUAD_ROWS * a + r:P:QUAD, :],
+                                  in_=scale_rows[first + r: first + BLOCKS: QUAD_ROWS, :])
+            load_words(query_table[a], tab2_words[a])
 
         wg_f32 = {}
 
@@ -153,26 +125,41 @@ def tile_list_beam_sigmoid_glu_kernel(tc, tab_words, tab_scales, tab2_words, tab
 
         load_wg(0, 0)
         load_wg(0, 1)
-        nc.sync.dma_start(out=w4_codes, in_=w4_words.rearrange("b p e -> p b e").bitcast(I32))
-        for r in range(QUAD_ROWS):
-            nc.sync.dma_start(out=w4_planes[r:P:QUAD, :, :],
-                              in_=w4_scales[:, r:BLOCKS:QUAD_ROWS, :].rearrange("b q n -> q b n").bitcast(I32))
-        load_wg(1, 0)
-        load_wg(1, 1)
-        load_wg(2, 0)
-        load_wg(2, 1)
+        nc.sync.dma_start(out=w4_codes[:], in_=w4_words.rearrange("b p e -> p b e").bitcast(I32))
+        for c in range(1, CHUNKS):
+            for b in range(PASSES):
+                load_wg(c, b)
 
-        att = [tile("att%d" % q, [P, PASSES, QUARTER, PACK], F32) for q in range(QUARTERS)]
-        h_bf = [tile("h_bf%d" % q, [P, PASSES, QUARTER * PACK], BF16) for q in range(QUARTERS)]
-        h_codes = [tile("h_codes%d" % h, [P, PASSES * HALF], U32) for h in range(HALVES)]
-        h_plane = [tile("h_plane%d" % h, [P, PASSES * HALF], U8) for h in range(HALVES)]
+        identity = tile("identity", [P, P], F32)
+        make_identity(nc, identity[:])
+        conf_bank = psum.tile([P, S2], F32, name="bank%d" % CONF_BANK)
+        for u in range(PASSES * PACK):
+            b, t = divmod(u, PACK)
+            nc.tensor.transpose(conf_bank[:, u: u + P],
+                                conf_row[:, PASS_LEN * b + t: PASS_LEN * (b + 1): PACK], identity[:])
+
+        keys = [tile("keys%d" % a, [P, S], U32) for a in range(PASSES)]
+        queries = [tile("queries%d" % a, [P, S2], U32) for a in range(PASSES)]
+        for a in range(PASSES):
+            nc.vector.tensor_copy(keys[a][:].rearrange("p (b t m) -> p b m t", b=PASSES, t=PACK),
+                                  key_table[a][:].bitcast(U32).indirect(key_list[:]))
+        for a, width in enumerate((QUARTER, QUARTER)):
+            for first in range(0, S2, width):
+                nc.vector.tensor_copy(
+                    queries[a][:, first: first + width],
+                    query_table[a][:].bitcast(U32).indirect(
+                        query_list[:, first // LIST_GROUP: (first + width) // LIST_GROUP]))
+
+        att = {(b, q): tile("att%d_%d" % (b, q), [P, QUARTER, PACK], F32)
+               for b in range(PASSES) for q in range(QUARTERS)}
+        h_bf = {(b, half): tile("h_bf%d_%d" % (b, half), [P, HALF * PACK], BF16)
+                for b in range(PASSES) for half in range(2)}
+        h_codes = [tile("h_codes%d" % b, [P, S2], U32) for b in range(PASSES)]
+        h_plane = [tile("h_plane%d" % b, [P, S2], U8) for b in range(PASSES)]
         pieces = [(c, b) for c in range(CHUNKS) for b in range(PASSES)]
-        wg_bf = {(c, b): tile("wg_bf%d_%d" % (c, b), [P, CHUNK * PACK], BF16)
-                 for c, b in pieces if (c, b) not in SPLIT}
-        wg_bf.update({(c, b, m): tile("wg_bf%d_%d_%d" % (c, b, m), [P, P * PACK], BF16)
-                      for c, b in SPLIT for m in range(CHUNK // P)})
         wg_codes = {(c, b): tile("wg_codes%d_%d" % (c, b), [P, CHUNK], U32) for c, b in pieces}
         wg_plane = {(c, b): tile("wg_plane%d_%d" % (c, b), [P, CHUNK], U8) for c, b in pieces}
+        wg_bf = {}
 
         def score_pass(acc, b, q, a):
             plane = planes[a][QUAD_ROWS * a:, :].bitcast(U8)
@@ -186,141 +173,136 @@ def tile_list_beam_sigmoid_glu_kernel(tc, tab_words, tab_scales, tab2_words, tab
                     rhs_scale=plane[:, S + QUARTER * q: S + QUARTER * (q + 1)],
                     start=(a == 0 and t == 0), stop=(a == PASSES - 1 and t == PACK - 1))
 
-        def h_cols(q, b):
-            first = HALF * b + QUARTER * (q % 2)
-            return slice(first, first + QUARTER)
+        def weigh(b, q):
+            width = QUARTER * PACK
+            dst = h_bf[b, q // 2][:, width * (q % 2): width * (q % 2 + 1)]
+            factor = conf_bank[:, PACK * b: PACK * (b + 1)].unsqueeze(1).to_broadcast([P, QUARTER, PACK])
+            nc.vector.tensor_tensor(dst.rearrange("p (j t) -> p j t", t=PACK), att[b, q][:], factor, MULT)
 
-        def weigh(q):
-            factor = conf_bank[:, :PASSES * PACK].rearrange("p (b t) -> p b t", t=PACK).unsqueeze(2).to_broadcast([P, PASSES, QUARTER, PACK])
-            nc.vector.tensor_tensor(h_bf[q][:].rearrange("p b (j t) -> p b j t", t=PACK), att[q][:], factor, MULT)
+        def quantise_h(b, half):
+            cols = slice(HALF * half, HALF * (half + 1))
+            nc.vector.quantize_mx(out=h_codes[b][:, cols].bitcast(FP8X4), scales=h_plane[b][:, cols],
+                                  in_=h_bf[b, half][:])
 
-        def quantise_h(q):
-            for b in range(PASSES):
-                nc.vector.quantize_mx(out=h_codes[q // 2][:, h_cols(q, b)].bitcast(FP8X4),
-                                      scales=h_plane[q // 2][:, h_cols(q, b)], in_=h_bf[q][:, b, :])
+        def span(m, tiles):
+            return slice(P * (m % 2), P * (m % 2 + tiles))
 
-        def channels(piece):
-            return slice(0, CHUNK) if len(piece) == 2 else slice(P * piece[2], P * (piece[2] + 1))
+        def round_wg(engine, m, b, tiles):
+            wg_bf[m, b] = tile("wg_bf%d_%d" % (m, b), [P, tiles * P * PACK], BF16)
+            src = wg_f32[m // 2, b][:, :, span(m, tiles)]
+            if engine == "gpsimd":
+                nc.gpsimd.tensor_scalar(wg_bf[m, b][:].rearrange("p (x t) -> p x t", t=PACK),
+                                        src.rearrange("p t x -> p x t"), 1.0, 0.0, MULT, ADD)
+            else:
+                copy = nc.vector.tensor_copy if engine == "vector" else nc.scalar.copy
+                copy(wg_bf[m, b][:].rearrange("p (x y t) -> p x t y", y=RUN, t=PACK),
+                     src.rearrange("p t (x y) -> p x t y", y=RUN))
 
-        def quantise_wg(*piece):
-            nc.vector.quantize_mx(out=wg_codes[piece[:2]][:, channels(piece)].bitcast(FP8X4),
-                                  scales=wg_plane[piece[:2]][:, channels(piece)], in_=wg_bf[piece][:])
+        def quantise_wg(m, b):
+            cols = span(m, wg_bf[m, b].shape[1] // (P * PACK))
+            nc.vector.quantize_mx(out=wg_codes[m // 2, b][:, cols].bitcast(FP8X4),
+                                  scales=wg_plane[m // 2, b][:, cols], in_=wg_bf[m, b][:])
 
-        def round_wg(copy, *piece):
-            copy(wg_bf[piece][:].rearrange("p (x y t) -> p x t y", y=RUN, t=PACK),
-                 wg_f32[piece[:2]][:, :, channels(piece)].rearrange("p t (x y) -> p x t y", y=RUN))
+        def gate_pass(acc, m, b):
+            nc.tensor.matmul_mx(
+                out=acc[:], lhsT=wg_codes[m // 2, b][:, span(m, 1)].bitcast(FP8X4),
+                lhsT_scale=wg_plane[m // 2, b][:, span(m, 1)],
+                rhs=h_codes[b][:].bitcast(FP8X4), rhs_scale=h_plane[b][:], start=(b == 0), stop=(b == 1))
 
-        def round_on_gpsimd(*piece):
-            nc.gpsimd.tensor_scalar(wg_bf[piece][:].rearrange("p (x t) -> p x t", t=PACK),
-                                    wg_f32[piece[:2]][:, :, channels(piece)].rearrange("p t x -> p x t"),
-                                    1.0, 0.0, MULT, ADD)
+        def context_pass(acc, m, b, cols):
+            n0 = P * m
+            nc.tensor.matmul_mx(
+                out=acc[:, cols],
+                lhsT=w4_codes[:, b, n0 // 2: (n0 + P) // 2].bitcast(U8).bitcast(FP4X4),
+                lhsT_scale=w4_planes[:, b, n0 // BYTES_PER_I32: (n0 + P) // BYTES_PER_I32].bitcast(U8),
+                rhs=h_codes[b][:, cols].bitcast(FP8X4), rhs_scale=h_plane[b][:, cols],
+                start=(b == 0 and cols.start == 0), stop=(b == 1 and cols.stop == S2))
 
-        def gate(h, c, acc):
-            for m in range(CHUNK // P):
-                for b in range(PASSES):
-                    cols = slice(P * m, P * (m + 1))
-                    picked = slice(HALF * b, HALF * (b + 1))
-                    nc.tensor.matmul_mx(
-                        out=acc[:, HALF * m: HALF * (m + 1)],
-                        lhsT=wg_codes[c, b][:, cols].bitcast(FP8X4), lhsT_scale=wg_plane[c, b][:, cols],
-                        rhs=h_codes[h][:, picked].bitcast(FP8X4), rhs_scale=h_plane[h][:, picked],
-                        start=(b == 0), stop=(b == PASSES - 1))
+        gate_sig = {}
 
-        def context(q, c, acc):
-            for m in range(CHUNK // P):
-                n0 = CHUNK * c + P * m
-                first = HALF * m + QUARTER * (q % 2)
-                for b in range(PASSES):
-                    nc.tensor.matmul_mx(
-                        out=acc[:, first: first + QUARTER],
-                        lhsT=w4_codes[:, b, n0 // 2: (n0 + P) // 2].bitcast(U8).bitcast(FP4X4),
-                        lhsT_scale=w4_planes[:, b, n0 // BYTES_PER_I32: (n0 + P) // BYTES_PER_I32].bitcast(U8),
-                        rhs=h_codes[q // 2][:, h_cols(q, b)].bitcast(FP8X4), rhs_scale=h_plane[q // 2][:, h_cols(q, b)],
-                        start=(b == 0), stop=(b == PASSES - 1))
+        def gate_sigmoid(m, cols=slice(0, S2)):
+            gate_sig[m, cols.start] = tile("gate_sig%d_%d" % (m, cols.start), [P, cols.stop - cols.start], F32)
+            nc.scalar.activation(gate_sig[m, cols.start][:], gates[m][:, cols], SIGMOID)
 
-        def finish(name, gate_sum, context_sum, dst):
-            gate_sig = tile("gate_sig" + name, [P, gate_sum.shape[1]], F32)
-            result = tile("result" + name, [P, gate_sum.shape[1]], F32)
-            nc.scalar.activation(gate_sig[:], gate_sum, SIGMOID)
-            nc.vector.tensor_tensor(result[:], context_sum, gate_sig[:], MULT)
-            nc.sync.dma_start(out=dst, in_=result[:].rearrange("p (m j) -> p m j", j=HALF))
+        def finish(m, cols=slice(0, S2)):
+            result = tile("result%d_%d" % (m, cols.start), [P, cols.stop - cols.start], F32)
+            nc.vector.tensor_tensor(result[:], contexts[m][:, cols], gate_sig[m, cols.start][:], MULT)
+            nc.sync.dma_start(out=out[P * m: P * (m + 1), cols], in_=result[:])
 
-        def out_rows(h, c):
-            return out[CHUNK * c: CHUNK * (c + 1), HALF * h: HALF * (h + 1)].rearrange("(m p) j -> p m j", p=P)
+        for b in range(PASSES):
+            for q in range(QUARTERS):
+                acc = bank(q)
+                for a in range(PASSES):
+                    score_pass(acc, b, q, a)
+                nc.scalar.activation(att[b, q][:], acc[:].rearrange("p (t j) -> p j t", t=PACK), SIGMOID)
 
-        scores = [(q, b) for q in range(QUARTERS) for b in range(PASSES)]
-        for number, (q, b) in enumerate(scores):
-            acc = bank(number % SCORE_BANKS)
-            for a in range(PASSES):
-                score_pass(acc, b, q, a)
-            nc.scalar.activation(att[q][:, b, :, :], acc[:].rearrange("p (t j) -> p j t", t=PACK), SIGMOID)
+        low, high = slice(0, HALF), slice(HALF, S2)
+        context_banks = (4, 5, 6, 0, 1, 4)
+        gate_banks = (2, 3, CONF_BANK, 2, 3, CONF_BANK)
+        early = TILES - 1
+        contexts, gates = {}, {}
 
-        free = list(range(SCORE_BANKS, BANKS - 1))
-        free.extend(number % SCORE_BANKS for number in range(len(scores) - SCORE_BANKS, len(scores)))
-        free.append(BANKS - 1)
-        sums = {}
-
-        def sum_bank(step, h, c):
-            if (step, h, c) not in sums:
-                number = free.pop(0)
-                sums[step, h, c] = (number, bank(number))
-            return sums[step, h, c][1]
-
-        def do_gate(h, c):
-            gate(h, c, sum_bank(gate, h, c))
-
-        def do_context(q, c):
-            context(q, c, sum_bank(context, q // 2, c))
-
-        def finish_unit(h, c):
-            finish("%d_%d" % (h, c), sums[gate, h, c][1][:], sums[context, h, c][1][:], out_rows(h, c))
-            free.extend((sums[gate, h, c][0], sums[context, h, c][0]))
-
-        on_vector, on_scalar = nc.vector.tensor_copy, nc.scalar.copy
-        round_wg(on_vector, 0, 0)
+        round_wg("gpsimd", 0, 0, 2)
+        for q in range(3):
+            weigh(0, q)
+        quantise_h(0, 0)
+        round_wg("gpsimd", 0, 1, 2)
+        for m in range(early):
+            contexts[m] = bank(context_banks[m])
+            context_pass(contexts[m], m, 0, low)
+        weigh(0, 3)
+        weigh(1, 0)
+        weigh(1, 1)
         quantise_wg(0, 0)
-        round_on_gpsimd(0, 1)
-        weigh(0)
-        weigh(1)
-        for q in range(2):
-            quantise_h(q)
-            for c in range(CHUNKS):
-                do_context(q, c)
-        round_on_gpsimd(1, 0, 0)
-        round_wg(on_scalar, 1, 1)
-        round_wg(on_scalar, 2, 0)
-        weigh(2)
+        quantise_h(0, 1)
+        quantise_h(1, 0)
+        for m in range(early):
+            context_pass(contexts[m], m, 0, high)
+        round_wg("scalar", 2, 0, 2)
+        round_wg("scalar", 2, 1, 1)
+        round_wg("gpsimd", 3, 1, 1)
+        round_wg("scalar", 4, 0, 2)
+        for m in range(2):
+            gates[m] = bank(gate_banks[m])
+            gate_pass(gates[m], m, 0)
+        for m in range(early):
+            context_pass(contexts[m], m, 1, low)
+        weigh(1, 2)
+        weigh(1, 3)
         quantise_wg(0, 1)
-        do_gate(0, 0)
-        quantise_h(2)
-        round_on_gpsimd(1, 0, 1)
-        for c in range(CHUNKS):
-            do_context(2, c)
-        weigh(3)
-        quantise_wg(1, 0, 0)
-        quantise_h(3)
-        do_gate(1, 0)
-        do_context(3, 0)
-        quantise_wg(1, 0, 1)
-        quantise_wg(1, 1)
-        finish_unit(0, 0)
-        round_wg(on_vector, 2, 1, 1)
-        round_wg(on_scalar, 2, 1, 0)
-        do_gate(0, 1)
-        do_gate(1, 1)
-        do_context(3, 1)
+        quantise_h(1, 1)
+        for m in range(2):
+            gate_pass(gates[m], m, 1)
+            gate_sigmoid(m)
+            context_pass(contexts[m], m, 1, high)
         quantise_wg(2, 0)
-        quantise_wg(2, 1, 1)
-        quantise_wg(2, 1, 0)
-        finish_unit(1, 0)
-        do_gate(0, 2)
-        do_gate(1, 2)
-        do_context(3, 2)
-        finish_unit(0, 1)
-        finish_unit(1, 1)
-        c = CHUNKS - 1
-        for h in range(HALVES):
-            for m in range(CHUNK // P):
-                cols = slice(HALF * m, HALF * (m + 1))
-                finish("%d_%d_%d" % (h, c, m), sums[gate, h, c][1][:, cols], sums[context, h, c][1][:, cols],
-                       out_rows(h, c)[:, m: m + 1, :])
+        quantise_wg(2, 1)
+        quantise_wg(3, 1)
+        round_wg("vector", 5, 1, 1)
+        quantise_wg(4, 0)
+        round_wg("gpsimd", 4, 1, 1)
+        for m in range(2, 4):
+            gates[m] = bank(gate_banks[m])
+            for b in range(PASSES):
+                gate_pass(gates[m], m, b)
+            gate_sigmoid(m)
+            context_pass(contexts[m], m, 1, high)
+        context_pass(contexts[4], 4, 1, high)
+        for m in range(2):
+            finish(m)
+            gates[4 + m] = bank(gate_banks[4 + m])
+            gate_pass(gates[4 + m], 4 + m, 0)
+        quantise_wg(5, 1)
+        quantise_wg(4, 1)
+        gate_pass(gates[4], 4, 1)
+        gate_pass(gates[5], 5, 1)
+        contexts[early] = bank(context_banks[early])
+        for b in range(PASSES):
+            context_pass(contexts[early], early, b, slice(0, S2))
+        gate_sigmoid(4)
+        for cols in (low, high):
+            gate_sigmoid(5, cols)
+        for m in range(2, 5):
+            finish(m)
+        for cols in (low, high):
+            finish(5, cols)

@@ -34,11 +34,13 @@ QUARTER = S2 // QUARTERS
 RUN = 2
 SCORE_BANKS = 4
 CONF_BANK = 7
+KEY_HEAD = 3 * T // 4
 TILES = N // P
 CHUNK = 2 * P
 CHUNKS = N // CHUNK
 
 REUSES = {
+    "wg_bf0_0": "query_table1",
     "h_codes0": "wg_f32_0_0",
     "wg_bf0_1": "h_bf0_0",
     "wg_plane0_0": "wg_f32_0_1",
@@ -83,8 +85,8 @@ def tile_list_beam_sigmoid_glu_kernel(tc, tab_words, tab_scales, tab2_words, tab
         for a in range(PASSES):
             nc.vector.memset(planes[a][:], 0)
 
-        def load_words(dst, words):
-            nc.sync.dma_start(out=dst[:], in_=words.rearrange("p t i -> p (t i)").bitcast(I32))
+        def load_words(dst, words, cols):
+            nc.sync.dma_start(out=dst[:, cols], in_=words.rearrange("p t i -> p (t i)").bitcast(I32)[:, cols])
 
         def load_scale_rows(dst, scales):
             nc.sync.dma_start(out=dst[:SCALE_ROWS, :], in_=scales.rearrange("a q t -> (a q) t").bitcast(I32))
@@ -93,9 +95,9 @@ def tile_list_beam_sigmoid_glu_kernel(tc, tab_words, tab_scales, tab2_words, tab
         nc.sync.dma_start(key_list[:], offs)
         load_scale_rows(query_scale_table, tab2_scales)
         nc.sync.dma_start(query_list[:], offs2)
-        load_words(key_table[0], tab_words[0])
+        load_words(key_table[0], tab_words[0], slice(0, T))
         nc.sync.dma_start(out=conf_row[:1, :], in_=conf.rearrange("(o i) -> o i", o=1))
-        load_words(key_table[1], tab_words[1])
+        load_words(key_table[1], tab_words[1], slice(0, KEY_HEAD))
         for r in range(QUAD_ROWS):
             nc.gpsimd.dma_start(out=w4_planes[r:P:QUAD, :, :],
                                 in_=w4_scales[:, r:BLOCKS:QUAD_ROWS, :].rearrange("b q n -> q b n").bitcast(I32))
@@ -109,12 +111,17 @@ def tile_list_beam_sigmoid_glu_kernel(tc, tab_words, tab_scales, tab2_words, tab
                               key_scales[:].rearrange("p (b m t) -> p b t m", b=PASSES, t=PACK))
         nc.vector.tensor_copy(scale_rows[:, S // BYTES_PER_I32:], query_scales[:].bitcast(I32))
 
-        for a in range(PASSES):
+        def move_to_planes(a):
             first = BLOCKS * a
             for r in range(QUAD_ROWS):
                 nc.sync.dma_start(out=planes[a][QUAD_ROWS * a + r:P:QUAD, :],
                                   in_=scale_rows[first + r: first + BLOCKS: QUAD_ROWS, :])
-            load_words(query_table[a], tab2_words[a])
+
+        move_to_planes(0)
+        load_words(key_table[1], tab_words[1], slice(KEY_HEAD, T))
+        load_words(query_table[0], tab2_words[0], slice(0, T2))
+        move_to_planes(1)
+        load_words(query_table[1], tab2_words[1], slice(0, T2))
 
         wg_f32 = {}
 

@@ -40,13 +40,15 @@ CHUNK = 2 * P
 CHUNKS = N // CHUNK
 
 REUSES = {
-    "wg_bf0_0": "query_table1",
-    "h_codes0": "wg_f32_0_0",
+    "h_codes0_0": "wg_f32_0_0",
+    "h_codes0_1": "wg_f32_0_1",
+    "wg_plane0_1": "att1_2",
     "wg_bf0_1": "h_bf0_0",
-    "wg_plane0_0": "wg_f32_0_1",
+    "wg_plane0_0": "att1_1",
     "h_bf1_1": "h_bf0_1",
     "wg_bf3_1": "h_bf1_0",
-    "wg_bf4_1": "wg_bf4_0",
+    "wg_bf5_1": "wg_bf4_1",
+    "gate_sig0_0": "wg_f32_4_0",
 }
 
 
@@ -75,15 +77,15 @@ def tile_list_beam_sigmoid_glu_kernel(tc, tab_words, tab_scales, tab2_words, tab
         planes = [tile("planes%d" % a, [P, (S + S2) // BYTES_PER_I32], I32) for a in range(PASSES)]
         w4_codes = tile("w4_codes", [P, PASSES, N // 2], I32)
         w4_planes = tile("w4_planes", [P, PASSES, N // BYTES_PER_I32], I32)
-        conf_row = tile("conf_row", [P, S], F32)
+        conf_sb = tile("conf_sb", [P, P], F32)
 
         for rows in (slice(QUAD, 2 * QUAD), slice(2 * QUAD, P)):
             nc.vector.memset(key_scale_table[rows, :], 0)
             nc.gpsimd.memset(query_scale_table[rows, :], 0)
-        nc.gpsimd.memset(conf_row[:], 0.0)
         nc.gpsimd.memset(w4_planes[:], 0)
         for a in range(PASSES):
             nc.vector.memset(planes[a][:], 0)
+        nc.vector.memset(conf_sb[:, PASSES * PACK:], 0.0)
 
         def load_words(dst, words, cols):
             nc.sync.dma_start(out=dst[:, cols], in_=words.rearrange("p t i -> p (t i)").bitcast(I32)[:, cols])
@@ -95,12 +97,10 @@ def tile_list_beam_sigmoid_glu_kernel(tc, tab_words, tab_scales, tab2_words, tab
         nc.sync.dma_start(key_list[:], offs)
         load_scale_rows(query_scale_table, tab2_scales)
         nc.sync.dma_start(query_list[:], offs2)
+        nc.sync.dma_start(out=conf_sb[:, :PASSES * PACK].rearrange("p (b t) -> p b t", t=PACK),
+                          in_=conf.rearrange("(b p t) -> p b t", b=PASSES, t=PACK))
         load_words(key_table[0], tab_words[0], slice(0, T))
-        nc.sync.dma_start(out=conf_row[:1, :], in_=conf.rearrange("(o i) -> o i", o=1))
         load_words(key_table[1], tab_words[1], slice(0, KEY_HEAD))
-        for r in range(QUAD_ROWS):
-            nc.gpsimd.dma_start(out=w4_planes[r:P:QUAD, :, :],
-                                in_=w4_scales[:, r:BLOCKS:QUAD_ROWS, :].rearrange("b q n -> q b n").bitcast(I32))
 
         key_scales = tile("key_scales", [P, S], U8)
         query_scales = tile("query_scales", [P, S2], U8)
@@ -125,44 +125,63 @@ def tile_list_beam_sigmoid_glu_kernel(tc, tab_words, tab_scales, tab2_words, tab
 
         wg_f32 = {}
 
-        def load_wg(c, b):
-            wg_f32[c, b] = tile("wg_f32_%d_%d" % (c, b), [P, PACK, CHUNK], F32)
-            rows = wg[PASS_LEN * b: PASS_LEN * (b + 1), CHUNK * c: CHUNK * (c + 1)]
-            nc.sync.dma_start(out=wg_f32[c, b][:], in_=rows.rearrange("(p t) n -> p t n", t=PACK))
+        def load_wg(m, b, tiles):
+            piece = tile("wg_f32_%d_%d" % (m, b), [P, PACK, tiles * P], F32)
+            rows = wg[PASS_LEN * b: PASS_LEN * (b + 1), P * m: P * (m + tiles)]
+            nc.sync.dma_start(out=piece[:], in_=rows.rearrange("(p t) n -> p t n", t=PACK))
+            for k in range(tiles):
+                wg_f32[m + k, b] = (piece, P * k)
 
-        load_wg(0, 0)
-        load_wg(0, 1)
+        load_wg(0, 0, 2)
+        load_wg(0, 1, 2)
         nc.sync.dma_start(out=w4_codes[:], in_=w4_words.rearrange("b p e -> p b e").bitcast(I32))
-        for c in range(1, CHUNKS):
-            for b in range(PASSES):
-                load_wg(c, b)
+        for r in range(QUAD_ROWS):
+            nc.sync.dma_start(out=w4_planes[r:P:QUAD, :, :],
+                              in_=w4_scales[:, r:BLOCKS:QUAD_ROWS, :].rearrange("b q n -> q b n").bitcast(I32))
+        load_wg(2, 0, 2)
+        load_wg(2, 1, 2)
+        load_wg(4, 0, 2)
+        load_wg(4, 1, 1)
+        load_wg(5, 1, 1)
 
         identity = tile("identity", [P, P], F32)
         make_identity(nc, identity[:])
-        conf_bank = psum.tile([P, S2], F32, name="bank%d" % CONF_BANK)
-        for u in range(PASSES * PACK):
-            b, t = divmod(u, PACK)
-            nc.tensor.transpose(conf_bank[:, u: u + P],
-                                conf_row[:, PASS_LEN * b + t: PASS_LEN * (b + 1): PACK], identity[:])
+        turned = bank(CONF_BANK - 1)
+        nc.tensor.transpose(turned[:, :P], conf_sb[:], identity[:])
+        conf_rows = tile("conf_rows", [P, P], F32)
+        nc.vector.tensor_copy(conf_rows[:], turned[:, :P])
+        conf_bank = bank(CONF_BANK)
+        nc.tensor.transpose(conf_bank[:, :P], conf_rows[:], identity[:])
 
         keys = [tile("keys%d" % a, [P, S], U32) for a in range(PASSES)]
         queries = [tile("queries%d" % a, [P, S2], U32) for a in range(PASSES)]
         for a in range(PASSES):
             nc.vector.tensor_copy(keys[a][:].rearrange("p (b t m) -> p b m t", b=PASSES, t=PACK),
                                   key_table[a][:].bitcast(U32).indirect(key_list[:]))
-        for a, width in enumerate((QUARTER, QUARTER)):
-            for first in range(0, S2, width):
+        for a in range(PASSES):
+            for first, last in ((0, QUARTER), (QUARTER, HALF), (HALF, S2)):
                 nc.vector.tensor_copy(
-                    queries[a][:, first: first + width],
-                    query_table[a][:].bitcast(U32).indirect(
-                        query_list[:, first // LIST_GROUP: (first + width) // LIST_GROUP]))
+                    queries[a][:, first: last],
+                    query_table[a][:].bitcast(U32).indirect(query_list[:, first // LIST_GROUP: last // LIST_GROUP]))
 
         att = {(b, q): tile("att%d_%d" % (b, q), [P, QUARTER, PACK], F32)
                for b in range(PASSES) for q in range(QUARTERS)}
         h_bf = {(b, half): tile("h_bf%d_%d" % (b, half), [P, HALF * PACK], BF16)
                 for b in range(PASSES) for half in range(2)}
-        h_codes = [tile("h_codes%d" % b, [P, S2], U32) for b in range(PASSES)]
-        h_plane = [tile("h_plane%d" % b, [P, S2], U8) for b in range(PASSES)]
+        first_codes = [tile("h_codes0_%d" % half, [P, HALF], U32) for half in range(2)]
+        first_plane = [tile("h_plane0_%d" % half, [P, HALF], U8) for half in range(2)]
+        second_codes = tile("h_codes1", [P, S2], U32)
+        second_plane = tile("h_plane1", [P, S2], U8)
+
+        def h_operand(b, cols):
+            if b == 0:
+                return first_codes[cols.start // HALF][:], first_plane[cols.start // HALF][:]
+            return second_codes[:, cols], second_plane[:, cols]
+
+        def h_parts(b, cols):
+            width = HALF if b == 0 else cols.stop - cols.start
+            return [slice(first, first + width) for first in range(cols.start, cols.stop, width)]
+
         pieces = [(c, b) for c in range(CHUNKS) for b in range(PASSES)]
         wg_codes = {(c, b): tile("wg_codes%d_%d" % (c, b), [P, CHUNK], U32) for c, b in pieces}
         wg_plane = {(c, b): tile("wg_plane%d_%d" % (c, b), [P, CHUNK], U8) for c, b in pieces}
@@ -187,16 +206,16 @@ def tile_list_beam_sigmoid_glu_kernel(tc, tab_words, tab_scales, tab2_words, tab
             nc.vector.tensor_tensor(dst.rearrange("p (j t) -> p j t", t=PACK), att[b, q][:], factor, MULT)
 
         def quantise_h(b, half):
-            cols = slice(HALF * half, HALF * (half + 1))
-            nc.vector.quantize_mx(out=h_codes[b][:, cols].bitcast(FP8X4), scales=h_plane[b][:, cols],
-                                  in_=h_bf[b, half][:])
+            codes, plane = h_operand(b, slice(HALF * half, HALF * (half + 1)))
+            nc.vector.quantize_mx(out=codes.bitcast(FP8X4), scales=plane, in_=h_bf[b, half][:])
 
         def span(m, tiles):
             return slice(P * (m % 2), P * (m % 2 + tiles))
 
         def round_wg(engine, m, b, tiles):
             wg_bf[m, b] = tile("wg_bf%d_%d" % (m, b), [P, tiles * P * PACK], BF16)
-            src = wg_f32[m // 2, b][:, :, span(m, tiles)]
+            piece, first = wg_f32[m, b]
+            src = piece[:, :, first: first + tiles * P]
             if engine == "gpsimd":
                 nc.gpsimd.tensor_scalar(wg_bf[m, b][:].rearrange("p (x t) -> p x t", t=PACK),
                                         src.rearrange("p t x -> p x t"), 1.0, 0.0, MULT, ADD)
@@ -210,20 +229,24 @@ def tile_list_beam_sigmoid_glu_kernel(tc, tab_words, tab_scales, tab2_words, tab
             nc.vector.quantize_mx(out=wg_codes[m // 2, b][:, cols].bitcast(FP8X4),
                                   scales=wg_plane[m // 2, b][:, cols], in_=wg_bf[m, b][:])
 
-        def gate_pass(acc, m, b):
-            nc.tensor.matmul_mx(
-                out=acc[:], lhsT=wg_codes[m // 2, b][:, span(m, 1)].bitcast(FP8X4),
-                lhsT_scale=wg_plane[m // 2, b][:, span(m, 1)],
-                rhs=h_codes[b][:].bitcast(FP8X4), rhs_scale=h_plane[b][:], start=(b == 0), stop=(b == 1))
+        def gate_pass(acc, m, b, cols=slice(0, S2)):
+            for part in h_parts(b, cols):
+                codes, plane = h_operand(b, part)
+                nc.tensor.matmul_mx(
+                    out=acc[:, part], lhsT=wg_codes[m // 2, b][:, span(m, 1)].bitcast(FP8X4),
+                    lhsT_scale=wg_plane[m // 2, b][:, span(m, 1)], rhs=codes.bitcast(FP8X4), rhs_scale=plane,
+                    start=(b == 0 and part.start == 0), stop=(b == 1 and part.stop == S2))
 
         def context_pass(acc, m, b, cols):
             n0 = P * m
-            nc.tensor.matmul_mx(
-                out=acc[:, cols],
-                lhsT=w4_codes[:, b, n0 // 2: (n0 + P) // 2].bitcast(U8).bitcast(FP4X4),
-                lhsT_scale=w4_planes[:, b, n0 // BYTES_PER_I32: (n0 + P) // BYTES_PER_I32].bitcast(U8),
-                rhs=h_codes[b][:, cols].bitcast(FP8X4), rhs_scale=h_plane[b][:, cols],
-                start=(b == 0 and cols.start == 0), stop=(b == 1 and cols.stop == S2))
+            for part in h_parts(b, cols):
+                codes, plane = h_operand(b, part)
+                nc.tensor.matmul_mx(
+                    out=acc[:, part],
+                    lhsT=w4_codes[:, b, n0 // 2: (n0 + P) // 2].bitcast(U8).bitcast(FP4X4),
+                    lhsT_scale=w4_planes[:, b, n0 // BYTES_PER_I32: (n0 + P) // BYTES_PER_I32].bitcast(U8),
+                    rhs=codes.bitcast(FP8X4), rhs_scale=plane,
+                    start=(b == 0 and part.start == 0), stop=(b == 1 and part.stop == S2))
 
         gate_sig = {}
 
@@ -260,8 +283,8 @@ def tile_list_beam_sigmoid_glu_kernel(tc, tab_words, tab_scales, tab2_words, tab
         weigh(0, 3)
         weigh(1, 0)
         weigh(1, 1)
-        quantise_wg(0, 0)
         quantise_h(0, 1)
+        quantise_wg(0, 0)
         quantise_h(1, 0)
         for m in range(early):
             context_pass(contexts[m], m, 0, high)
@@ -285,9 +308,10 @@ def tile_list_beam_sigmoid_glu_kernel(tc, tab_words, tab_scales, tab2_words, tab
         quantise_wg(2, 0)
         quantise_wg(2, 1)
         quantise_wg(3, 1)
-        round_wg("vector", 5, 1, 1)
+        round_wg("vector", 4, 1, 1)
         quantise_wg(4, 0)
-        round_wg("gpsimd", 4, 1, 1)
+        quantise_wg(4, 1)
+        round_wg("gpsimd", 5, 1, 1)
         for m in range(2, 4):
             gates[m] = bank(gate_banks[m])
             for b in range(PASSES):
@@ -295,17 +319,18 @@ def tile_list_beam_sigmoid_glu_kernel(tc, tab_words, tab_scales, tab2_words, tab
             gate_sigmoid(m)
             context_pass(contexts[m], m, 1, high)
         context_pass(contexts[4], 4, 1, high)
-        for m in range(2):
-            finish(m)
-            gates[4 + m] = bank(gate_banks[4 + m])
-            gate_pass(gates[4 + m], 4 + m, 0)
+        finish(0)
+        finish(1)
         quantise_wg(5, 1)
-        quantise_wg(4, 1)
-        gate_pass(gates[4], 4, 1)
-        gate_pass(gates[5], 5, 1)
+        gates[4] = bank(gate_banks[4])
+        for b in range(PASSES):
+            gate_pass(gates[4], 4, b)
+        gates[5] = bank(gate_banks[5])
+        gate_pass(gates[5], 5, 0)
         contexts[early] = bank(context_banks[early])
         for b in range(PASSES):
             context_pass(contexts[early], early, b, slice(0, S2))
+        gate_pass(gates[5], 5, 1)
         gate_sigmoid(4)
         for cols in (low, high):
             gate_sigmoid(5, cols)

@@ -40,15 +40,18 @@ CHUNK = 2 * P
 CHUNKS = N // CHUNK
 
 REUSES = {
+    "wg_bf0_0": "wg_f32_128_0",
     "h_codes0_0": "wg_f32_0_0",
-    "h_codes0_1": "wg_f32_0_1",
-    "wg_plane0_1": "att1_2",
     "wg_bf0_1": "h_bf0_0",
+    "h_codes0_1": "wg_f32_0_1",
     "wg_plane0_0": "att1_1",
     "h_bf1_1": "h_bf0_1",
-    "wg_bf3_1": "h_bf1_0",
-    "wg_bf5_1": "wg_bf4_1",
-    "gate_sig0_0": "wg_f32_4_0",
+    "wg_bf448_1": "h_bf1_0",
+    "wg_plane0_1": "att1_2",
+    "wg_bf640_1": "wg_bf512_1",
+    "gate_sig0_0": "wg_f32_512_0",
+    "result0_0": "wg_f32_512_1",
+    "result3_0": "wg_f32_640_1",
 }
 
 
@@ -126,21 +129,24 @@ def tile_list_beam_sigmoid_glu_kernel(tc, tab_words, tab_scales, tab2_words, tab
         wg_f32 = {}
 
         def load_wg(m, b, tiles):
-            piece = tile("wg_f32_%d_%d" % (m, b), [P, PACK, tiles * P], F32)
+            piece = tile("wg_f32_%d_%d" % (P * m, b), [P, PACK, tiles * P], F32)
             rows = wg[PASS_LEN * b: PASS_LEN * (b + 1), P * m: P * (m + tiles)]
             nc.sync.dma_start(out=piece[:], in_=rows.rearrange("(p t) n -> p t n", t=PACK))
             for k in range(tiles):
-                wg_f32[m + k, b] = (piece, P * k)
+                wg_f32[m + k, b] = (piece, P * m)
 
-        load_wg(0, 0, 2)
-        load_wg(0, 1, 2)
+        load_wg(1, 0, 1)
+        load_wg(0, 0, 1)
+        load_wg(0, 1, 1)
+        load_wg(1, 1, 1)
         nc.sync.dma_start(out=w4_codes[:], in_=w4_words.rearrange("b p e -> p b e").bitcast(I32))
         for r in range(QUAD_ROWS):
             nc.sync.dma_start(out=w4_planes[r:P:QUAD, :, :],
                               in_=w4_scales[:, r:BLOCKS:QUAD_ROWS, :].rearrange("b q n -> q b n").bitcast(I32))
         load_wg(2, 0, 2)
         load_wg(2, 1, 2)
-        load_wg(4, 0, 2)
+        load_wg(4, 0, 1)
+        load_wg(5, 0, 1)
         load_wg(4, 1, 1)
         load_wg(5, 1, 1)
 
@@ -212,22 +218,22 @@ def tile_list_beam_sigmoid_glu_kernel(tc, tab_words, tab_scales, tab2_words, tab
         def span(m, tiles):
             return slice(P * (m % 2), P * (m % 2 + tiles))
 
-        def round_wg(engine, m, b, tiles):
-            wg_bf[m, b] = tile("wg_bf%d_%d" % (m, b), [P, tiles * P * PACK], BF16)
-            piece, first = wg_f32[m, b]
-            src = piece[:, :, first: first + tiles * P]
+        def round_wg(engine, n0, b, width):
+            wg_bf[n0, b] = tile("wg_bf%d_%d" % (n0, b), [P, width * PACK], BF16)
+            piece, first = wg_f32[n0 // P, b]
+            src = piece[:, :, n0 - first: n0 - first + width]
             if engine == "gpsimd":
-                nc.gpsimd.tensor_scalar(wg_bf[m, b][:].rearrange("p (x t) -> p x t", t=PACK),
+                nc.gpsimd.tensor_scalar(wg_bf[n0, b][:].rearrange("p (x t) -> p x t", t=PACK),
                                         src.rearrange("p t x -> p x t"), 1.0, 0.0, MULT, ADD)
             else:
                 copy = nc.vector.tensor_copy if engine == "vector" else nc.scalar.copy
-                copy(wg_bf[m, b][:].rearrange("p (x y t) -> p x t y", y=RUN, t=PACK),
+                copy(wg_bf[n0, b][:].rearrange("p (x y t) -> p x t y", y=RUN, t=PACK),
                      src.rearrange("p t (x y) -> p x t y", y=RUN))
 
-        def quantise_wg(m, b):
-            cols = span(m, wg_bf[m, b].shape[1] // (P * PACK))
-            nc.vector.quantize_mx(out=wg_codes[m // 2, b][:, cols].bitcast(FP8X4),
-                                  scales=wg_plane[m // 2, b][:, cols], in_=wg_bf[m, b][:])
+        def quantise_wg(n0, b):
+            cols = slice(n0 % CHUNK, n0 % CHUNK + wg_bf[n0, b].shape[1] // PACK)
+            nc.vector.quantize_mx(out=wg_codes[n0 // CHUNK, b][:, cols].bitcast(FP8X4),
+                                  scales=wg_plane[n0 // CHUNK, b][:, cols], in_=wg_bf[n0, b][:])
 
         def gate_pass(acc, m, b, cols=slice(0, S2)):
             for part in h_parts(b, cols):
@@ -272,11 +278,12 @@ def tile_list_beam_sigmoid_glu_kernel(tc, tab_words, tab_scales, tab2_words, tab
         early = TILES - 1
         contexts, gates = {}, {}
 
-        round_wg("gpsimd", 0, 0, 2)
+        round_wg("vector", 128, 0, 128)
+        round_wg("gpsimd", 0, 0, 128)
         for q in range(3):
             weigh(0, q)
         quantise_h(0, 0)
-        round_wg("gpsimd", 0, 1, 2)
+        round_wg("gpsimd", 0, 1, 128)
         for m in range(early):
             contexts[m] = bank(context_banks[m])
             context_pass(contexts[m], m, 0, low)
@@ -284,14 +291,17 @@ def tile_list_beam_sigmoid_glu_kernel(tc, tab_words, tab_scales, tab2_words, tab
         weigh(1, 0)
         weigh(1, 1)
         quantise_h(0, 1)
+        quantise_wg(128, 0)
         quantise_wg(0, 0)
         quantise_h(1, 0)
         for m in range(early):
             context_pass(contexts[m], m, 0, high)
-        round_wg("scalar", 2, 0, 2)
-        round_wg("scalar", 2, 1, 1)
-        round_wg("gpsimd", 3, 1, 1)
-        round_wg("scalar", 4, 0, 2)
+        round_wg("scalar", 128, 1, 128)
+        round_wg("scalar", 256, 0, 256)
+        round_wg("scalar", 256, 1, 128)
+        round_wg("scalar", 384, 1, 64)
+        round_wg("gpsimd", 448, 1, 64)
+        round_wg("scalar", 512, 0, 128)
         for m in range(2):
             gates[m] = bank(gate_banks[m])
             gate_pass(gates[m], m, 0)
@@ -300,18 +310,22 @@ def tile_list_beam_sigmoid_glu_kernel(tc, tab_words, tab_scales, tab2_words, tab
         weigh(1, 2)
         weigh(1, 3)
         quantise_wg(0, 1)
+        quantise_wg(128, 1)
         quantise_h(1, 1)
         for m in range(2):
             gate_pass(gates[m], m, 1)
             gate_sigmoid(m)
             context_pass(contexts[m], m, 1, high)
-        quantise_wg(2, 0)
-        quantise_wg(2, 1)
-        quantise_wg(3, 1)
-        round_wg("vector", 4, 1, 1)
-        quantise_wg(4, 0)
-        quantise_wg(4, 1)
-        round_wg("gpsimd", 5, 1, 1)
+        quantise_wg(256, 0)
+        quantise_wg(256, 1)
+        quantise_wg(384, 1)
+        quantise_wg(448, 1)
+        round_wg("vector", 640, 0, 128)
+        round_wg("vector", 512, 1, 128)
+        quantise_wg(512, 0)
+        quantise_wg(640, 0)
+        quantise_wg(512, 1)
+        round_wg("gpsimd", 640, 1, 128)
         for m in range(2, 4):
             gates[m] = bank(gate_banks[m])
             for b in range(PASSES):
@@ -321,20 +335,21 @@ def tile_list_beam_sigmoid_glu_kernel(tc, tab_words, tab_scales, tab2_words, tab
         context_pass(contexts[4], 4, 1, high)
         finish(0)
         finish(1)
-        quantise_wg(5, 1)
+        finish(2)
+        quantise_wg(640, 1)
         gates[4] = bank(gate_banks[4])
         for b in range(PASSES):
             gate_pass(gates[4], 4, b)
-        gates[5] = bank(gate_banks[5])
-        gate_pass(gates[5], 5, 0)
         contexts[early] = bank(context_banks[early])
         for b in range(PASSES):
             context_pass(contexts[early], early, b, slice(0, S2))
-        gate_pass(gates[5], 5, 1)
+        gates[5] = bank(gate_banks[5])
+        for b in range(PASSES):
+            gate_pass(gates[5], 5, b)
         gate_sigmoid(4)
         for cols in (low, high):
             gate_sigmoid(5, cols)
-        for m in range(2, 5):
+        for m in range(3, 5):
             finish(m)
         for cols in (low, high):
             finish(5, cols)

@@ -40,6 +40,7 @@ CHUNK = 2 * P
 CHUNKS = N // CHUNK
 
 REUSES = {
+    "keys1": "query_table0",
     "wg_bf0_0": "wg_f32_128_0",
     "h_codes0_0": "wg_f32_0_0",
     "wg_bf0_1": "h_bf0_0",
@@ -161,14 +162,21 @@ def tile_list_beam_sigmoid_glu_kernel(tc, tab_words, tab_scales, tab2_words, tab
 
         keys = [tile("keys%d" % a, [P, S], U32) for a in range(PASSES)]
         queries = [tile("queries%d" % a, [P, S2], U32) for a in range(PASSES)]
-        for a in range(PASSES):
-            nc.vector.tensor_copy(keys[a][:].rearrange("p (b t m) -> p b m t", b=PASSES, t=PACK),
-                                  key_table[a][:].bitcast(U32).indirect(key_list[:]))
-        for a in range(PASSES):
+        listed_keys = tile("listed_keys", [P, S], U32)
+
+        def gather_queries(a):
             for first, last in ((0, QUARTER), (QUARTER, HALF), (HALF, S2)):
                 nc.vector.tensor_copy(
                     queries[a][:, first: last],
                     query_table[a][:].bitcast(U32).indirect(query_list[:, first // LIST_GROUP: last // LIST_GROUP]))
+
+        nc.vector.tensor_copy(keys[0][:].rearrange("p (b t m) -> p b m t", b=PASSES, t=PACK),
+                              key_table[0][:].bitcast(U32).indirect(key_list[:]))
+        nc.vector.tensor_copy(listed_keys[:], key_table[1][:].bitcast(U32).indirect(key_list[:]))
+        gather_queries(0)
+        nc.vector.tensor_copy(keys[1][:].rearrange("p (b t x y) -> p b x t y", b=PASSES, t=PACK, y=PACK),
+                              listed_keys[:].rearrange("p (b x y t) -> p b x t y", b=PASSES, t=PACK, y=PACK))
+        gather_queries(1)
 
         att = {(b, q): tile("att%d_%d" % (b, q), [P, QUARTER, PACK], F32)
                for b in range(PASSES) for q in range(QUARTERS)}

@@ -39,7 +39,10 @@ TILES = N // P
 CHUNK = 2 * P
 CHUNKS = N // CHUNK
 
+QUERY_ROWS = slice(2 * QUAD, 3 * QUAD)
+
 REUSES = {
+    "keys0": "key_scale_table",
     "keys1": "query_table0",
     "wg_bf0_0": "wg_f32_128_0",
     "h_codes0_0": "wg_f32_0_0",
@@ -85,6 +88,7 @@ def tile_list_beam_sigmoid_glu_kernel(tc, tab_words, tab_scales, tab2_words, tab
 
         for rows in (slice(QUAD, 2 * QUAD), slice(2 * QUAD, P)):
             nc.vector.memset(key_scale_table[rows, :], 0)
+        for rows in (slice(0, 2 * QUAD), slice(3 * QUAD, P)):
             nc.gpsimd.memset(query_scale_table[rows, :], 0)
         nc.gpsimd.memset(w4_planes[:], 0)
         for a in range(PASSES):
@@ -95,14 +99,14 @@ def tile_list_beam_sigmoid_glu_kernel(tc, tab_words, tab_scales, tab2_words, tab
             nc.sync.dma_start(out=dst[:, cols], in_=words.rearrange("p t i -> p (t i)").bitcast(I32)[:, cols])
 
         def load_scale_rows(dst, scales):
-            nc.sync.dma_start(out=dst[:SCALE_ROWS, :], in_=scales.rearrange("a q t -> (a q) t").bitcast(I32))
+            nc.scalar.dma_start(out=dst, in_=scales.rearrange("a q t -> (a q) t").bitcast(I32))
 
-        load_scale_rows(key_scale_table, tab_scales)
+        load_scale_rows(key_scale_table[:SCALE_ROWS, :], tab_scales)
         nc.sync.dma_start(key_list[:], offs)
-        load_scale_rows(query_scale_table, tab2_scales)
+        load_scale_rows(query_scale_table[QUERY_ROWS, :], tab2_scales)
         nc.sync.dma_start(query_list[:], offs2)
-        nc.sync.dma_start(out=conf_sb[:, :PASSES * PACK].rearrange("p (b t) -> p b t", t=PACK),
-                          in_=conf.rearrange("(b p t) -> p b t", b=PASSES, t=PACK))
+        nc.scalar.dma_start(out=conf_sb[:, :PASSES * PACK].rearrange("p (b t) -> p b t", t=PACK),
+                            in_=conf.rearrange("(b p t) -> p b t", b=PASSES, t=PACK))
         load_words(key_table[0], tab_words[0], slice(0, T))
         load_words(key_table[1], tab_words[1], slice(0, KEY_HEAD))
 
@@ -113,7 +117,8 @@ def tile_list_beam_sigmoid_glu_kernel(tc, tab_words, tab_scales, tab2_words, tab
         nc.vector.tensor_copy(query_scales[:], query_scale_table[:].bitcast(U8).indirect(query_list[:]))
         nc.vector.tensor_copy(scale_rows[:].bitcast(U8)[:, :S].rearrange("p (b t m) -> p b t m", b=PASSES, t=PACK),
                               key_scales[:].rearrange("p (b m t) -> p b t m", b=PASSES, t=PACK))
-        nc.vector.tensor_copy(scale_rows[:, S // BYTES_PER_I32:], query_scales[:].bitcast(I32))
+        nc.vector.tensor_copy(scale_rows[:SCALE_ROWS, S // BYTES_PER_I32:],
+                              query_scales[:].bitcast(I32)[QUERY_ROWS, :])
 
         def move_to_planes(a):
             first = BLOCKS * a

from contextlib import ExitStack

import concourse.mybir as mybir
from concourse.masks import make_identity

K, T, S, T2, S2, N = 1024, 4096, 1024, 2048, 512, 768
FLOPS = 2 * K * S * S2 + 2 * 2 * S * N * S2

F32 = mybir.dt.float32
BF16 = mybir.dt.bfloat16
I32 = mybir.dt.int32
U32 = mybir.dt.uint32
U16 = mybir.dt.uint16
U8 = mybir.dt.uint8
FP8X4 = mybir.dt.float8_e4m3fn_x4
FP4X4 = mybir.dt.float4_e2m1fn_x4
SIGMOID = mybir.ActivationFunctionType.Sigmoid
MULT = mybir.AluOpType.mult
ADD = mybir.AluOpType.add

P = 128
PACK = 4
PASSES = 2
PASS_LEN = P * PACK
BLOCKS = 16
QUAD = 32
QUAD_ROWS = 4
SCALE_ROWS = PASSES * BLOCKS
LIST_GROUP = 16
BYTES_PER_I32 = 4
HALF = S2 // 2
QUARTERS = 4
QUARTER = S2 // QUARTERS
RUN = 2
SCORE_BANKS = 4
CONF_BANK = 7
KEY_HEAD = 3 * T // 4
TILES = N // P
CHUNK = 2 * P
CHUNKS = N // CHUNK

QUERY_ROWS = slice(2 * QUAD, 3 * QUAD)

REUSES = {
    "keys0": "key_scale_table",
    "keys1": "query_table0",
    "wg_bf0_0": "wg_f32_128_0",
    "h_codes0_0": "wg_f32_0_0",
    "wg_bf0_1": "h_bf0_0",
    "h_codes0_1": "wg_f32_0_1",
    "wg_plane0_0": "att1_1",
    "h_bf1_1": "h_bf0_1",
    "wg_bf448_1": "h_bf1_0",
    "wg_plane0_1": "att1_2",
    "wg_bf640_1": "wg_bf512_1",
    "gate_sig0_0": "wg_f32_512_0",
    "result0_0": "wg_f32_512_1",
    "result3_0": "wg_f32_640_1",
}


def tile_list_beam_sigmoid_glu_kernel(tc, tab_words, tab_scales, tab2_words, tab2_scales,
                                                   w4_words, w4_scales, wg, conf, offs, offs2, out):
    nc = tc.nc
    with ExitStack() as ctx:
        keep = ctx.enter_context(tc.tile_pool(name="keep", bufs=1))
        psum = ctx.enter_context(tc.psum_pool(name="psum", bufs=1))

        def owner(name):
            return owner(REUSES[name]) if name in REUSES else name

        def tile(name, shape, dtype):
            return keep.tile(shape, dtype, name=name, tag=owner(name), align_bytes=256)

        def bank(number):
            return psum.tile([P, S2], F32, name="bank%d" % number)

        key_list = keep.tile([P, S // LIST_GROUP], U16, name="key_list")
        query_list = keep.tile([P, S2 // LIST_GROUP], U16, name="query_list")
        key_table = [tile("key_table%d" % a, [P, T], I32) for a in range(PASSES)]
        query_table = [tile("query_table%d" % a, [P, T2], I32) for a in range(PASSES)]
        key_scale_table = tile("key_scale_table", [P, T // BYTES_PER_I32], I32)
        query_scale_table = tile("query_scale_table", [P, T2 // BYTES_PER_I32], I32)
        planes = [tile("planes%d" % a, [P, (S + S2) // BYTES_PER_I32], I32) for a in range(PASSES)]
        w4_codes = tile("w4_codes", [P, PASSES, N // 2], I32)
        w4_planes = tile("w4_planes", [P, PASSES, N // BYTES_PER_I32], I32)
        conf_sb = tile("conf_sb", [P, P], F32)

        for rows in (slice(QUAD, 2 * QUAD), slice(2 * QUAD, P)):
            nc.vector.memset(key_scale_table[rows, :], 0)
        for rows in (slice(0, 2 * QUAD), slice(3 * QUAD, P)):
            nc.gpsimd.memset(query_scale_table[rows, :], 0)
        nc.gpsimd.memset(w4_planes[:], 0)
        for a in range(PASSES):
            nc.vector.memset(planes[a][:], 0)
        nc.vector.memset(conf_sb[:, PASSES * PACK:], 0.0)

        def load_words(dst, words, cols):
            nc.sync.dma_start(out=dst[:, cols], in_=words.rearrange("p t i -> p (t i)").bitcast(I32)[:, cols])

        def load_scale_rows(dst, scales):
            nc.scalar.dma_start(out=dst, in_=scales.rearrange("a q t -> (a q) t").bitcast(I32))

        load_scale_rows(key_scale_table[:SCALE_ROWS, :], tab_scales)
        nc.sync.dma_start(key_list[:], offs)
        load_scale_rows(query_scale_table[QUERY_ROWS, :], tab2_scales)
        nc.sync.dma_start(query_list[:], offs2)
        nc.scalar.dma_start(out=conf_sb[:, :PASSES * PACK].rearrange("p (b t) -> p b t", t=PACK),
                            in_=conf.rearrange("(b p t) -> p b t", b=PASSES, t=PACK))
        load_words(key_table[0], tab_words[0], slice(0, T))
        load_words(key_table[1], tab_words[1], slice(0, KEY_HEAD))

        key_scales = tile("key_scales", [P, S], U8)
        query_scales = tile("query_scales", [P, S2], U8)
        scale_rows = tile("scale_rows", [P, (S + S2) // BYTES_PER_I32], I32)
        nc.vector.tensor_copy(key_scales[:], key_scale_table[:].bitcast(U8).indirect(key_list[:]))
        nc.vector.tensor_copy(query_scales[:], query_scale_table[:].bitcast(U8).indirect(query_list[:]))
        nc.vector.tensor_copy(scale_rows[:].bitcast(U8)[:, :S].rearrange("p (b t m) -> p b t m", b=PASSES, t=PACK),
                              key_scales[:].rearrange("p (b m t) -> p b t m", b=PASSES, t=PACK))
        nc.vector.tensor_copy(scale_rows[:SCALE_ROWS, S // BYTES_PER_I32:],
                              query_scales[:].bitcast(I32)[QUERY_ROWS, :])

        def move_to_planes(a):
            first = BLOCKS * a
            for r in range(QUAD_ROWS):
                nc.sync.dma_start(out=planes[a][QUAD_ROWS * a + r:P:QUAD, :],
                                  in_=scale_rows[first + r: first + BLOCKS: QUAD_ROWS, :])

        move_to_planes(0)
        load_words(key_table[1], tab_words[1], slice(KEY_HEAD, T))
        load_words(query_table[0], tab2_words[0], slice(0, T2))
        move_to_planes(1)
        load_words(query_table[1], tab2_words[1], slice(0, T2))

        wg_f32 = {}

        def load_wg(m, b, tiles):
            piece = tile("wg_f32_%d_%d" % (P * m, b), [P, PACK, tiles * P], F32)
            rows = wg[PASS_LEN * b: PASS_LEN * (b + 1), P * m: P * (m + tiles)]
            nc.sync.dma_start(out=piece[:], in_=rows.rearrange("(p t) n -> p t n", t=PACK))
            for k in range(tiles):
                wg_f32[m + k, b] = (piece, P * m)

        load_wg(1, 0, 1)
        load_wg(0, 0, 1)
        load_wg(0, 1, 1)
        load_wg(1, 1, 1)
        nc.sync.dma_start(out=w4_codes[:], in_=w4_words.rearrange("b p e -> p b e").bitcast(I32))
        for r in range(QUAD_ROWS):
            nc.sync.dma_start(out=w4_planes[r:P:QUAD, :, :],
                              in_=w4_scales[:, r:BLOCKS:QUAD_ROWS, :].rearrange("b q n -> q b n").bitcast(I32))
        load_wg(2, 0, 2)
        load_wg(2, 1, 2)
        load_wg(4, 0, 1)
        load_wg(5, 0, 1)
        load_wg(4, 1, 1)
        load_wg(5, 1, 1)

        identity = tile("identity", [P, P], F32)
        make_identity(nc, identity[:])
        turned = bank(CONF_BANK - 1)
        nc.tensor.transpose(turned[:, :P], conf_sb[:], identity[:])
        conf_rows = tile("conf_rows", [P, P], F32)
        nc.vector.tensor_copy(conf_rows[:], turned[:, :P])
        conf_bank = bank(CONF_BANK)
        nc.tensor.transpose(conf_bank[:, :P], conf_rows[:], identity[:])

        keys = [tile("keys%d" % a, [P, S], U32) for a in range(PASSES)]
        queries = [tile("queries%d" % a, [P, S2], U32) for a in range(PASSES)]
        listed_keys = tile("listed_keys", [P, S], U32)

        def gather_queries(a):
            for first, last in ((0, QUARTER), (QUARTER, HALF), (HALF, S2)):
                nc.vector.tensor_copy(
                    queries[a][:, first: last],
                    query_table[a][:].bitcast(U32).indirect(query_list[:, first // LIST_GROUP: last // LIST_GROUP]))

        nc.vector.tensor_copy(keys[0][:].rearrange("p (b t m) -> p b m t", b=PASSES, t=PACK),
                              key_table[0][:].bitcast(U32).indirect(key_list[:]))
        nc.vector.tensor_copy(listed_keys[:], key_table[1][:].bitcast(U32).indirect(key_list[:]))
        gather_queries(0)
        nc.vector.tensor_copy(keys[1][:].rearrange("p (b t x y) -> p b x t y", b=PASSES, t=PACK, y=PACK),
                              listed_keys[:].rearrange("p (b x y t) -> p b x t y", b=PASSES, t=PACK, y=PACK))
        gather_queries(1)

        att = {(b, q): tile("att%d_%d" % (b, q), [P, QUARTER, PACK], F32)
               for b in range(PASSES) for q in range(QUARTERS)}
        h_bf = {(b, half): tile("h_bf%d_%d" % (b, half), [P, HALF * PACK], BF16)
                for b in range(PASSES) for half in range(2)}
        first_codes = [tile("h_codes0_%d" % half, [P, HALF], U32) for half in range(2)]
        first_plane = [tile("h_plane0_%d" % half, [P, HALF], U8) for half in range(2)]
        second_codes = tile("h_codes1", [P, S2], U32)
        second_plane = tile("h_plane1", [P, S2], U8)

        def h_operand(b, cols):
            if b == 0:
                return first_codes[cols.start // HALF][:], first_plane[cols.start // HALF][:]
            return second_codes[:, cols], second_plane[:, cols]

        def h_parts(b, cols):
            width = HALF if b == 0 else cols.stop - cols.start
            return [slice(first, first + width) for first in range(cols.start, cols.stop, width)]

        pieces = [(c, b) for c in range(CHUNKS) for b in range(PASSES)]
        wg_codes = {(c, b): tile("wg_codes%d_%d" % (c, b), [P, CHUNK], U32) for c, b in pieces}
        wg_plane = {(c, b): tile("wg_plane%d_%d" % (c, b), [P, CHUNK], U8) for c, b in pieces}
        wg_bf = {}

        def score_pass(acc, b, q, a):
            plane = planes[a][QUAD_ROWS * a:, :].bitcast(U8)
            for t in range(PACK):
                u = PACK * b + t
                nc.tensor.matmul_mx(
                    out=acc[:, QUARTER * t: QUARTER * (t + 1)],
                    lhsT=keys[a][:, P * u: P * (u + 1)].bitcast(FP8X4),
                    lhsT_scale=plane[:, P * u: P * (u + 1)],
                    rhs=queries[a][:, QUARTER * q: QUARTER * (q + 1)].bitcast(FP8X4),
                    rhs_scale=plane[:, S + QUARTER * q: S + QUARTER * (q + 1)],
                    start=(a == 0 and t == 0), stop=(a == PASSES - 1 and t == PACK - 1))

        def weigh(b, q):
            width = QUARTER * PACK
            dst = h_bf[b, q // 2][:, width * (q % 2): width * (q % 2 + 1)]
            factor = conf_bank[:, PACK * b: PACK * (b + 1)].unsqueeze(1).to_broadcast([P, QUARTER, PACK])
            nc.vector.tensor_tensor(dst.rearrange("p (j t) -> p j t", t=PACK), att[b, q][:], factor, MULT)

        def quantise_h(b, half):
            codes, plane = h_operand(b, slice(HALF * half, HALF * (half + 1)))
            nc.vector.quantize_mx(out=codes.bitcast(FP8X4), scales=plane, in_=h_bf[b, half][:])

        def span(m, tiles):
            return slice(P * (m % 2), P * (m % 2 + tiles))

        def round_wg(engine, n0, b, width):
            wg_bf[n0, b] = tile("wg_bf%d_%d" % (n0, b), [P, width * PACK], BF16)
            piece, first = wg_f32[n0 // P, b]
            src = piece[:, :, n0 - first: n0 - first + width]
            if engine == "gpsimd":
                nc.gpsimd.tensor_scalar(wg_bf[n0, b][:].rearrange("p (x t) -> p x t", t=PACK),
                                        src.rearrange("p t x -> p x t"), 1.0, 0.0, MULT, ADD)
            else:
                copy = nc.vector.tensor_copy if engine == "vector" else nc.scalar.copy
                copy(wg_bf[n0, b][:].rearrange("p (x y t) -> p x t y", y=RUN, t=PACK),
                     src.rearrange("p t (x y) -> p x t y", y=RUN))

        def quantise_wg(n0, b):
            cols = slice(n0 % CHUNK, n0 % CHUNK + wg_bf[n0, b].shape[1] // PACK)
            nc.vector.quantize_mx(out=wg_codes[n0 // CHUNK, b][:, cols].bitcast(FP8X4),
                                  scales=wg_plane[n0 // CHUNK, b][:, cols], in_=wg_bf[n0, b][:])

        def gate_pass(acc, m, b, cols=slice(0, S2)):
            for part in h_parts(b, cols):
                codes, plane = h_operand(b, part)
                nc.tensor.matmul_mx(
                    out=acc[:, part], lhsT=wg_codes[m // 2, b][:, span(m, 1)].bitcast(FP8X4),
                    lhsT_scale=wg_plane[m // 2, b][:, span(m, 1)], rhs=codes.bitcast(FP8X4), rhs_scale=plane,
                    start=(b == 0 and part.start == 0), stop=(b == 1 and part.stop == S2))

        def context_pass(acc, m, b, cols):
            n0 = P * m
            for part in h_parts(b, cols):
                codes, plane = h_operand(b, part)
                nc.tensor.matmul_mx(
                    out=acc[:, part],
                    lhsT=w4_codes[:, b, n0 // 2: (n0 + P) // 2].bitcast(U8).bitcast(FP4X4),
                    lhsT_scale=w4_planes[:, b, n0 // BYTES_PER_I32: (n0 + P) // BYTES_PER_I32].bitcast(U8),
                    rhs=codes.bitcast(FP8X4), rhs_scale=plane,
                    start=(b == 0 and part.start == 0), stop=(b == 1 and part.stop == S2))

        gate_sig = {}

        def gate_sigmoid(m, cols=slice(0, S2)):
            gate_sig[m, cols.start] = tile("gate_sig%d_%d" % (m, cols.start), [P, cols.stop - cols.start], F32)
            nc.scalar.activation(gate_sig[m, cols.start][:], gates[m][:, cols], SIGMOID)

        def finish(m, cols=slice(0, S2)):
            result = tile("result%d_%d" % (m, cols.start), [P, cols.stop - cols.start], F32)
            nc.vector.tensor_tensor(result[:], contexts[m][:, cols], gate_sig[m, cols.start][:], MULT)
            nc.sync.dma_start(out=out[P * m: P * (m + 1), cols], in_=result[:])

        for b in range(PASSES):
            for q in range(QUARTERS):
                acc = bank(q)
                for a in range(PASSES):
                    score_pass(acc, b, q, a)
                nc.scalar.activation(att[b, q][:], acc[:].rearrange("p (t j) -> p j t", t=PACK), SIGMOID)

        low, high = slice(0, HALF), slice(HALF, S2)
        context_banks = (4, 5, 6, 0, 1, 4)
        gate_banks = (2, 3, CONF_BANK, 2, 3, CONF_BANK)
        early = TILES - 1
        contexts, gates = {}, {}

        round_wg("vector", 128, 0, 128)
        round_wg("gpsimd", 0, 0, 128)
        for q in range(3):
            weigh(0, q)
        quantise_h(0, 0)
        round_wg("gpsimd", 0, 1, 128)
        for m in range(early):
            contexts[m] = bank(context_banks[m])
            context_pass(contexts[m], m, 0, low)
        weigh(0, 3)
        weigh(1, 0)
        weigh(1, 1)
        quantise_h(0, 1)
        quantise_wg(128, 0)
        quantise_wg(0, 0)
        quantise_h(1, 0)
        for m in range(early):
            context_pass(contexts[m], m, 0, high)
        round_wg("scalar", 128, 1, 128)
        round_wg("scalar", 256, 0, 256)
        round_wg("scalar", 256, 1, 128)
        round_wg("scalar", 384, 1, 64)
        round_wg("gpsimd", 448, 1, 64)
        round_wg("scalar", 512, 0, 128)
        for m in range(2):
            gates[m] = bank(gate_banks[m])
            gate_pass(gates[m], m, 0)
        for m in range(early):
            context_pass(contexts[m], m, 1, low)
        weigh(1, 2)
        weigh(1, 3)
        quantise_wg(0, 1)
        quantise_wg(128, 1)
        quantise_h(1, 1)
        for m in range(2):
            gate_pass(gates[m], m, 1)
            gate_sigmoid(m)
            context_pass(contexts[m], m, 1, high)
        quantise_wg(256, 0)
        quantise_wg(256, 1)
        quantise_wg(384, 1)
        quantise_wg(448, 1)
        round_wg("vector", 640, 0, 128)
        round_wg("vector", 512, 1, 128)
        quantise_wg(512, 0)
        quantise_wg(640, 0)
        quantise_wg(512, 1)
        round_wg("gpsimd", 640, 1, 128)
        for m in range(2, 4):
            gates[m] = bank(gate_banks[m])
            for b in range(PASSES):
                gate_pass(gates[m], m, b)
            gate_sigmoid(m)
            context_pass(contexts[m], m, 1, high)
        context_pass(contexts[4], 4, 1, high)
        finish(0)
        finish(1)
        finish(2)
        quantise_wg(640, 1)
        gates[4] = bank(gate_banks[4])
        for b in range(PASSES):
            gate_pass(gates[4], 4, b)
        contexts[early] = bank(context_banks[early])
        for b in range(PASSES):
            context_pass(contexts[early], early, b, slice(0, S2))
        gates[5] = bank(gate_banks[5])
        for b in range(PASSES):
            gate_pass(gates[5], 5, b)
        gate_sigmoid(4)
        for cols in (low, high):
            gate_sigmoid(5, cols)
        for m in range(3, 5):
            finish(m)
        for cols in (low, high):
            finish(5, cols)
